import numpy as np, ml_dtypes
CORES = [1,5,17,21,33,37,49,53]
N = 8
BF = ml_dtypes.bfloat16
def gentries(a):
    return np.ascontiguousarray(a.reshape(8, 16, -1).transpose(0, 2, 1)).reshape(8, -1)
def gtable(e):
    e = np.asarray(e); return np.ascontiguousarray(e.reshape(8, -1, 16).transpose(0, 2, 1)).reshape(128, -1).astype(np.int32)
V, P, XC, B, RO = 128, 256, 8192, 64, 3
E = 16 * V
def place_record(n, a, p, t):
    return ((n * (2 * a + 1) >> 4) + n + 37 * p + 77 * t) & (XC - 1)
def seat(rng, ln, key=None, mix=True, pair=False):
    oc = np.full((N, 8, E), P, np.int64); qs = np.full((N, 8, 16 * P), E, np.int64)
    for r in range(N):
        for g in range(8):
            at = np.flatnonzero((np.arange(16) < ln[r, g][:, None]).reshape(-1))
            if pair and g & 1: at = at[np.argsort(2 * np.minimum(at, at ^ (16 * B)) + (at > (at ^ (16 * B))))]
            s = rng.permutation(16 * P) if key is None else np.argsort(key[r, g].reshape(-1))
            s = s[:len(at)]
            if mix: s = rng.permutation(s)
            oc[r, g, at] = s >> 4; qs[r, g, s] = at
    return oc, qs
def put(oc, qs, r, g, s, n):
    b = int(np.flatnonzero(qs[r, g] == n)[0]); m = int(qs[r, g, s])
    qs[r, g, s] = n; qs[r, g, b] = m; oc[r, g, m] = b >> 4; oc[r, g, n] = s >> 4
def aim(w, y, u):
    i = np.arange(1, 16)[:, None]
    w[0] = (u - np.sum(16 * i * w[1:] + np.minimum(w[1:], y[1:, None]), axis=0)) & (V - 1)
def pack(x, want, oc, qs, th):
    return {"x": np.ascontiguousarray(x.reshape(N, 128, XC)).astype(np.float32).astype(BF), "want": np.stack([want.reshape(128, P)] * N).astype(np.float32).astype(BF),
            "oc": np.stack([gtable(a) for a in oc]), "qs": np.stack([gtable(a) for a in qs]), "th": np.repeat(th, 16, axis=1).reshape(N, 128, 1).astype(np.int32)}
def goods(rng):
    return rng.integers(0, 256, (N, 8, 16, XC)), rng.integers(0, 256, (8, 16, P))
def setup_inputs(rng):
    x, want = goods(rng); oc, qs = seat(rng, rng.integers(8, 17, (N, 8, V)))
    return pack(x, want, oc, qs, rng.integers(450, 901, (N, 8)))
def setup_inputs_alike(rng):
    x, want = goods(rng); ln = rng.choice(np.array([16, 16, 8, 3, 12]), (N, 8, V))
    ln[:, 2] = 16; ln[:, 4] = rng.integers(12, 16, (N, V)); ln[:, 6] = rng.integers(12, 16, (N, V)); ln[:, 6, 1] = 16; ln[N - 1, 6, V - 1] = 15
    key = rng.random((N, 8, P, 1)) + 0.0001 * rng.random((N, 8, P, 16))
    oc, qs = seat(rng, ln, key, False, True)
    want[3] = want[3][:, :1]; x[N - 1, 5] = x[N - 1, 5] >> 1
    key = rng.random((N, 8, P, 16)); one = np.arange(16) == rng.integers(0, 16, (N, P, 1))
    key[:, 4] = np.where(one, -1, np.where(np.roll(one, 1, axis=2), 9, key[:, 4]))
    key[:, 6, 1:N + 1] = 9; key[:, 6, P - 1] = 9; key[N - 1, 6, P - 1, :15] = -1
    for r in range(N): key[r, 6, r + 1, r] = -1
    oc2, qs2 = seat(rng, ln, key)
    oc[:, 2:7:2] = oc2[:, 2:7:2]; qs[:, 2:7:2] = qs2[:, 2:7:2]
    n = np.arange(E); m = n ^ (16 * B)
    for r in range(N):
        a = np.where((n & 15) == 0, n >> 4, np.roll(oc[r, 2], 1)); c = place_record(m, a[m], oc[r, 2], 0)
        y = x[r, 2] >> 1; y[:, c] = y[:, c] | 128; x[r, 2] = y
        put(oc, qs, r, 6, 16 * (r + 1) + r, 128)
    for k in range(15): put(oc, qs, N - 1, 6, 16 * (P - 1) + k, E - 16 + k)
    y = rng.integers(0, 256, 16); y[0] = 255; x[:, 4] = y[:, None]; want[4] = want[4][:, :1]; aim(want[4], y, 0)
    u = 2 + rng.integers(0, V - 3, P); u[1:N + 1] = 1; u[P - 1] = V - 1
    x[:, 6] = 255; aim(want[6], np.full(16, 255), u)
    th = rng.integers(600, 1500, (N, 8)); th[:, 2] = 4080
    return pack(x, want, oc, qs, th)
def setup_inputs_ties(rng):
    x, want = goods(rng); x = 85 * (x >> 6); want = 85 * (want >> 6)
    oc, qs = seat(rng, rng.integers(8, 17, (N, 8, V)))
    for a in (x, oc, qs): a[:, ::2] = a[:1, ::2]
    x[0, 2] = np.minimum(x[0, 2], 170); x[0, 6] = np.minimum(x[0, 6], 170)
    return pack(x, want, oc, qs, 85 * rng.integers(4, 11, (N, 8)) - rng.integers(0, 2, (N, 8)))
def setup_inputs_corners(rng):
    x, want = goods(rng); ln = rng.choice(np.array([0, 1, 15, 16]), (N, 8, V))
    kind = rng.random((N, 8, 1, XC)); x = np.where(kind < 0.4, 255, np.where(kind < 0.5, 0, x))
    cls = rng.integers(0, 4, (8, 1, P)); kind = rng.random((8, 1, P)); many = np.full((8, 16, P), 255); many[:, 1:2] = 255 - cls
    want = np.where(kind < 0.6, many, np.where(kind < 0.7, 0, want))
    want[7, :, ::16] = 255; want[7, 7, ::16] = 254
    for g in range(8):
        x[:g % N, g, 0] = np.minimum(x[:g % N, g, 0], 254)
        for c in range(4): ln[:, g, (16 * 120 * 255 + 4080 - 17 * c) & (V - 1)] = (15, 0, 16, 1)[(g + c) & 3]
    ln[:, 7, V - 1] = 15; ln[:, 0, V - 1] = 16; ln[:, 7, 0] = 16
    c = rng.integers(0, 5, (N, 8, P, 1)); c[:, :, 4::9] = 3
    one = np.arange(16) == rng.integers(0, 16, (N, 8, P, 1))
    key = rng.random((N, 8, P, 1)) + 0.0001 * rng.random((N, 8, P, 16))
    key = key + np.where(c == 0, 0, np.where(c == 1, np.where(one, 3, 0), np.where(c == 2, np.where(one, -3, 3), np.where(c == 3, 6, 1))))
    key[N - 1, 7, 0] = np.where(np.arange(16) < 15, -1, 9)
    oc, qs = seat(rng, ln, key)
    th = rng.choice(np.array([0, 1, 1000, 2000, 4080]), (N, 8)); th[:, ::2] = 4080; th[:, 5] = 4079; th[:, 7] = 4080
    return pack(x, want, oc, qs, th)
def setup_inputs_ends(rng):
    v = np.arange(V); low = np.minimum(v, v ^ B)
    ln = np.where((rng.random((N, 8, V)) < 0.35)[..., low], 16, 0)
    for q in (0, V - 1): ln[..., q] = 16; ln[..., q ^ B] = 16
    who = rng.random((N, 8, P, 1)); who[:, :, 0] = -1; who[:, :, P - 1] = -1
    oc, qs = seat(rng, ln, who + 0.0001 * rng.random((N, 8, P, 16)))
    kind = rng.random((8, 1, P)); want = np.where(kind < 0.25, 255, np.where(kind < 0.4, 0, 255 * rng.integers(0, 2, (8, 16, P))))
    want[:, :, 0] = 255; want[:, :, P - 1] = 255; want[:, :, P // 2] = 0; want[:, :, P - 2] = 0
    kind = rng.random((N, 8, 1, XC)); x = np.where(kind < 0.3, 255, np.where(kind < 0.45, 0, 255 * rng.integers(0, 2, (N, 8, 16, XC))))
    x[..., 0] = 255; x[..., XC - 1] = 255
    for r in range(N):
        for g in range(8):
            put(oc, qs, r, g, 16 * P - 1, E - 1); put(oc, qs, r, g, 0, 0)
            x[r, g, :, int(place_record(E - 1, int(oc[r, g, E - 2]), P - 1, 0))] = 255
    th = np.where(rng.random((N, 8)) < 0.3, 0, 4080); th[:, 0] = 4080; th[:, 1] = 0; th[:, 7] = 4080
    return pack(x, want, oc, qs, th)
def setup_inputs_spread(rng):
    x = np.minimum((np.exp2(8 * rng.random((N, 8, 1, XC))) * rng.random((N, 8, 16, XC))).astype(np.int64), 255)
    want = np.minimum((np.exp2(2 + 6 * rng.random((8, 1, P))) * rng.random((8, 16, P))).astype(np.int64), 255)
    ln = np.minimum((17 * rng.random((N, 8, V)) ** rng.choice(np.array([0.3, 0.6, 1.0, 2.0]), (N, 8, 1))).astype(np.int64), 16)
    oc, qs = seat(rng, ln)
    return pack(x, want, oc, qs, np.minimum(np.exp2(12 * rng.random((N, 8))).astype(np.int64), 4080))
def check_inputs(d):
    bad = []
    for k, hi in (("x", 255), ("want", 255), ("oc", P), ("qs", E), ("th", 4080)):
        a = np.asarray(d[k]).astype(np.float64)
        if not np.all((a >= 0) & (a <= hi)): bad.append("range of " + k)
        elif not np.all(a == np.floor(a)): bad.append("whole numbers of " + k)
    w = np.asarray(d["want"]).astype(np.float32)
    if not np.all(w == w[:1]): bad.append("want alike on all ranks")
    t = np.asarray(d["th"]).reshape(N, 8, 16)
    if not np.all(t == t[:, :, :1]): bad.append("th alike in the rows of a group")
    if "range of oc" in bad or "range of qs" in bad: return bad
    o = np.stack([gentries(a) for a in d["oc"]]).astype(np.int64); q = np.stack([gentries(a) for a in d["qs"]]).astype(np.int64)
    b = (o < P).reshape(N, 8, V, 16)
    if np.any(b[..., 1:] & ~b[..., :-1]): bad.append("queues of oc without gaps")
    ok = True; person = np.arange(16 * P) >> 4
    for r in range(N):
        for g in range(8):
            n = np.bincount(q[r, g], minlength=E + 1)[:E]; back = np.full(E + 1, P, np.int64); back[q[r, g]] = person
            ok = ok and np.array_equal(n, (o[r, g] < P).astype(n.dtype)) and np.array_equal(back[:E], o[r, g])
    if not ok: bad.append("every occupied place of oc in just one slot of qs, of its person")
    return bad
def reference(x, want, oc, qs, th):
    xs = x.astype(np.float32).astype(np.int32).reshape(N, 8, 16, XC); ws = want.astype(np.float32).astype(np.int32).reshape(N, 8, 16, P)
    wp = np.concatenate([ws, np.zeros((N, 8, 16, 1), np.int32)], axis=3); wsum = np.add.reduce(16 * np.arange(16)[:, None] * ws.astype(np.int64), axis=2)
    o = np.stack([gentries(a) for a in oc]).astype(np.int64)
    q = np.stack([gentries(a) for a in qs]).astype(np.int64)
    lim = th.astype(np.int64).reshape(N, 8, 16)[:, :, :1]
    n = np.arange(E); mate = n ^ (16 * B); v = n >> 4; head = (n & 15) == 0; none = np.full((N, 8, 1), E, np.int64)
    for t in range(RO):
        occ = o < P; ahead = np.where(head, v, np.roll(o, 1, axis=2))
        w = np.take_along_axis(wp, o[:, :, None, :], 3)
        own = np.add.reduce(np.minimum(np.take_along_axis(xs, place_record(n, ahead, o, t)[:, :, None, :], 3), w), axis=2).astype(np.int64)
        other = np.add.reduce(np.minimum(np.take_along_axis(xs, place_record(mate, ahead[..., mate], o, t)[:, :, None, :], 3), w), axis=2).astype(np.int64)
        swap = occ & occ[..., mate] & (other + other[..., mate] > own + own[..., mate])
        o2 = np.where(swap, o[..., mate], o); c = np.where(swap, other[..., mate], own)
        qd = np.take_along_axis(np.concatenate([np.where(swap, mate, n), none], axis=2), q, 2)
        best = np.max(np.take_along_axis(np.concatenate([c, np.full((N, 8, 1), -1, np.int64)], axis=2), qd, 2).reshape(N, 8, P, 16), axis=3)
        top = np.max(best, axis=0); holder = np.argmax(best, axis=0)
        tp = np.concatenate([np.broadcast_to(top, (N, 8, P)), np.zeros((N, 8, 1), np.int64)], axis=2)
        go = (c < np.take_along_axis(tp, o2, 2) - lim) | (head & ((v & 7) == t))
        stay = (occ & ~go).astype(np.int64).reshape(N, 8, V, 16)
        to = np.where(stay == 1, 16 * np.arange(V)[:, None] + np.add.accumulate(stay, axis=3) - stay, E).reshape(N, 8, E)
        o = np.full((N, 8, E + 1), P, np.int64); np.put_along_axis(o, to, o2, 2); o = np.ascontiguousarray(o[..., :E])
        q = np.take_along_axis(np.concatenate([to, none], axis=2), qd, 2)
        ln = np.add.reduce(stay, axis=3); empty = q.reshape(N, 8, P, 16) == E; u = (wsum + top) & (V - 1)
        for r in range(N):
            for g in range(8):
                p = np.flatnonzero(np.any(empty[r, g], axis=1) & (top[g] >= 0) & (holder[g] == r)); p = p[ln[r, g, u[r, g, p]] < 16]
                k, i = np.unique(u[r, g, p], return_index=True); p = p[i]; at = 16 * k + ln[r, g, k]
                o[r, g, at] = p; q[r, g, 16 * p + np.argmax(empty[r, g, p], axis=1)] = at
    return {"yoc": np.stack([gtable(a) for a in o]).astype(np.float32), "yq": np.stack([gtable(a) for a in q]).astype(np.float32)}

@@ -1,0 +1,605 @@
+import math
+from concourse.bass import DstId, RemoteDMATransfer
+from concourse.mybir import AluOpType as OP, ActivationFunctionType as AF
+
+LN3 = math.log(3.0)
+F32, BF, H, I32, U16 = "float32", "bfloat16", "float16", "int32", "uint16"
+
+
+def _sb(dtype, **names):
+    return {n: ("sbuf", [128, w], dtype) for n, w in names.items()}
+
+
+SCRATCH = {}
+SCRATCH.update(_sb(BF, xs=8192, wn=272, gmb=128, lkb=2048, apb=128, bkb=2048, tri=128, i8=128, in8=128, qlm=128, lenm=128,
+                   trit=128, bs8=512, cneg=128, c16=128, k2=128, c77=256, trf=128, ihb=128, sm=64, ctb=256, on=128, rho=256,
+                   bsel=512, pmx=512, dm=256, ivb=128, hm=384, wg=2048, mn=4096, zd=4096, zf=4096, ze=2048, hfs=256,
+                   oh=2048, ub=256))
+SCRATCH.update(_sb(I32, oci=128, qsi=256, thi=1, cint=8, qi=256, qa=256, hz=256, hm13=256, zu=32))
+SCRATCH.update(_sb(U16, ol=128, ql=256, hu=256, ol2=128, clist=16, ul=16))
+SCRATCH.update(_sb(H, ih=128, sh=128, stmp=128, hcb=256, i37=128, pre=128, emp=128, sc=128, trie=128, cst=384, csl=384,
+                   k2l=128, o=128, cp=128, c2=128, o2=128, kb=256, st=128, e16=128, fr=2048, o3t=128, tof=128, em=256,
+                   qt=256))
+SCRATCH.update(_sb(F32, col=32, cI=128, cg=128, ck=128, c8=128, ipm=256, pv=256, bv=256, ch=32, cht=32, R=16, n8=128,
+                   sx=320, pc=48, of32=128, y1=128, sd=128, dw=2064, fw=2064, tsb=256, tm=256, land0=128, land1=128,
+                   land2=128, x2=256, ce=512, p16=160, kt=128, kp=16, wm=272, lna=160, apf=8, qp=128, corr=128, iseq=128,
+                   appl=128, qlw=128, l16=128, lv=128, tt=128, wmk=256, npl=256, fe=256, yo=128, yqs=256))
+del SCRATCH["pv"]
+PSUM = ("r0", "r1", "r2", "r3", "pa", "plo", "phi", "pq")
+SCRATCH.update({n: ("psum", [128, 512], F32) for n in PSUM})
+SEMAPHORES = ["cV", "cS", "cP", "cG", "d_oc", "d_qs", "d_wn", "d_th", "d_x", "d_yo", "d_yq", "arr0", "arr1", "arr2", "loc"]
+PART = {"pint": ("cint", 0, 1), "kint": ("cint", 1, 1), "gint": ("cint", 2, 1), "lint": ("cint", 3, 1), "hint": ("cint", 4, 1),
+        "dlo": ("sx", 0, 64), "dd": ("sx", 64, 64), "s": ("sx", 128, 64), "ml": ("sx", 192, 64), "dhi": ("sx", 256, 64),
+        "gc": ("sm", 0, 16), "ngc": ("sm", 16, 16), "wi": ("sm", 32, 16), "wts": ("sm", 48, 16), "gth": ("pc", 0, 16),
+        "thc": ("pc", 16, 16), "wsc": ("pc", 32, 16), "zi": ("zu", 0, 16), "ui": ("zu", 16, 16)}
+
+
+def rank_program(g, core, T, topo):
+    rank = T.rank_of(core)
+    if rank is None:
+        return
+    eng = {"V": g.vector, "S": g.scalar, "P": g.tensor, "G": g, "Y": g.sync}
+    count = {"V": 0, "S": 0, "P": 0, "G": 0}
+    known = {e: {} for e in eng}
+    snap = {}
+    hist = {}
+    bank = {}
+
+    def wait(e, ev):
+        if known[e].get(ev[0], 0) >= ev[1]:
+            return
+        eng[e].wait_ge(T.sem[ev[0]], ev[1])
+        for k, v in list(snap[ev].items()) + [ev]:
+            if known[e].get(k, 0) < v:
+                known[e][k] = v
+
+    def run(e, fn, reads, writes, sem=None, inc=1):
+        evs = []
+        for wr, regs in ((False, reads), (True, writes)):
+            for rg in regs:
+                b, lo, hi = rg[0], rg[1], rg[2]
+                if b in PSUM:
+                    evs += [v for k, v in bank.get(b, {}).items() if k != e]
+                else:
+                    evs += [a[3] for a in hist.get(b, []) if a[1] < hi and lo < a[2] and (wr or a[0])]
+        need = {}
+        for k, v in evs:
+            need[k] = max(need.get(k, 0), v)
+        for ev in sorted(need.items(), key=lambda q: -q[1]):
+            wait(e, ev)
+        if sem is None:
+            sem = "c" + e
+            count[e] += 1
+            ev = (sem, count[e])
+        else:
+            ev = (sem, inc)
+        fn().then_inc(T.sem[sem], inc)
+        snap[ev] = dict(known[e])
+        for wr, regs in ((False, reads), (True, writes)):
+            for rg in regs:
+                b, lo, hi = rg[0], rg[1], rg[2]
+                if b in PSUM:
+                    bank.setdefault(b, {})[e] = ev
+                else:
+                    h = hist.setdefault(b, [])
+                    if wr:
+                        h[:] = [a for a in h if not (lo <= a[1] and a[2] <= hi)]
+                    else:
+                        h[:] = [a for a in h if not (not a[0] and a[3][0] == ev[0] and a[1] == lo and a[2] == hi)]
+                    h.append((wr, lo, hi, ev))
+        return ev
+
+    def c(b, lo=None, hi=None, step=1):
+        n, at, w = PART.get(b) or (b, 0, SCRATCH[b][1][1])
+        if lo is None:
+            lo, hi = 0, w
+        return (n, at + lo, at + hi, step)
+
+    def ap(x):
+        if x[0] == "ind":
+            return ap(x[1]).indirect(ap(x[2]))
+        return T[x[0]][:, x[1]:x[2]:x[3]] if x[3] != 1 else T[x[0]][:, x[1]:x[2]]
+
+    def ind(w, o):
+        return ("ind", w, o)
+
+    def rd(*xs):
+        out = []
+        for x in xs:
+            if isinstance(x, tuple):
+                out += [x[1], x[2]] if x[0] == "ind" else [x]
+        return out
+
+    def val(x):
+        return ap(x) if isinstance(x, tuple) else x
+
+    def ts(out, a, s1, s2, o0, o1=None):
+        if o1 is None:
+            run("V", lambda: g.vector.tensor_scalar(ap(out), ap(a), val(s1), None, o0), rd(a, s1), [out])
+        else:
+            run("V", lambda: g.vector.tensor_scalar(ap(out), ap(a), val(s1), val(s2), o0, o1), rd(a, s1, s2), [out])
+
+    def tt(out, a, b, op):
+        run("V", lambda: g.vector.tensor_tensor(ap(out), ap(a), ap(b), op), rd(a, b), [out])
+
+    def cp(out, a):
+        run("V", lambda: g.vector.tensor_copy(ap(out), ap(a)), rd(a), [out])
+
+    def fill(out, v):
+        run("V", lambda: g.vector.memset(ap(out), v), [], [out])
+
+    def act(out, a, func, bias=0.0, scale=1.0):
+        run("S", lambda: g.scalar.activation(ap(out), ap(a), func, bias=val(bias), scale=val(scale)), rd(a, bias, scale), [out])
+
+    def mm(out, l, r, start, stop):
+        run("P", lambda: g.tensor.matmul(ap(out), ap(l), ap(r), start, stop), rd(l, r), [out])
+
+    def iota(out, pattern, base, cm):
+        small = SCRATCH[out[0]][2] != I32
+        if small:
+            run("G", lambda: g.iota(ap(out), pattern, base, cm, allow_small_or_imprecise_dtypes=True), [], [out])
+        else:
+            run("G", lambda: g.iota(ap(out), pattern, base, cm), [], [out])
+
+    def load(e, sem, b, hi, src):
+        run(e, lambda: eng[e].dma_start(T[b][:, 0:hi], src), [], [c(b, 0, hi)], sem=sem, inc=16)
+
+    def k_(b, k):
+        return c(b, 128 * k, 128 * k + 128)
+
+    PC, KC, GC, K8, BC, TH, THR, P64, W64, WX, PP, L3, LN, KX = [c("col", i, i + 1) for i in range(14)]
+    add, sub, mul, mx, mi, eq, ge, gt, lt = (OP.add, OP.subtract, OP.mult, OP.max, OP.min, OP.is_equal, OP.is_ge, OP.is_gt, OP.is_lt)
+
+    load("Y", "d_oc", "oci", 128, T.oc[:, :])
+    load("Y", "d_wn", "wn", 256, T.want[:, :])
+    load("Y", "d_x", "xs", 8192, T.x[:, :])
+    load("Y", "d_qs", "qsi", 256, T.qs[:, :])
+    load("Y", "d_th", "thi", 1, T.th[:, :])
+
+    iota(c("pint"), [[0, 1]], 0, 1)
+    iota(c("cI"), [[1, 128]], 0, 0)
+    iota(PC, [[0, 1]], 0, 1)
+    iota(c("cg"), [[1, 8], [0, 16]], 0, 0)
+    iota(c("ck"), [[0, 8], [1, 16]], 0, 0)
+    iota(c("c8"), [[0, 16], [1, 8]], 0, 0)
+    iota(c("ch"), [[0, 8], [64, 4]], 0, 0)
+    iota(c("bv"), [[0, 16], [1, 2], [0, 8]], 0, 0)
+    iota(c("ipm"), [[1, 256]], -256, 0)
+
+    fill(c("wn", 256, 272), 0.0)
+    fill(c("lkb"), 0.0)
+    fill(LN, 3.0)
+    fill(c("dw", 2048, 2064), 0.0)
+    fill(c("wm", 256, 272), 0.0)
+    ts(c("kint"), c("pint"), 15, None, OP.bitwise_and)
+    ts(c("gint"), c("pint"), 4, None, OP.arith_shift_right)
+    ts(c("lint"), c("pint"), 63, None, OP.bitwise_and)
+    ts(c("hint"), c("pint"), 6, None, OP.arith_shift_right)
+    cp(KC, c("kint"))
+    cp(GC, c("gint"))
+    cp(P64, c("lint"))
+    cp(W64, c("hint"))
+    ts(c("gmb"), c("cg"), GC, None, eq)
+    ts(c("ih"), c("cI"), PC, None, eq)
+    ts(c("R"), c("cI", 0, 16), KC, None, eq)
+    ts(K8, KC, 0.125, None, mul)
+    ts(c("stmp"), c("cI"), 1.0, PC, sub, eq)
+    ts(c("hcb", 0, 128), c("cI"), c("R", 0, 1), 8.5, mul, add)
+    ts(c("hcb", 128, 256), c("cI"), 0.0, -0.46875, mul, add)
+    tt(c("sh"), c("stmp"), c("gmb"), mul)
+    ts(c("i37"), c("ih"), 37.0, None, mul)
+    ts(c("n8"), c("cI"), 2.0, K8, mul, add)
+    cp(c("o"), c("oci"))
+    cp(c("ol"), c("oci"))
+    act(WX, P64, AF.Exp, 0.0, -LN3)
+    act(L3, LN, AF.Ln)
+    for k in range(16):
+        act(c("lkb", 128 * k + k, 128 * k + 128, 16), c("gmb", k, 128, 16), AF.Copy)
+    ts(c("pre"), c("cI"), 0.0, -2047.0, mul, add)
+
+    def h_consts(t):
+        mm(c("pa", 0, 256), c("ih"), c("hcb"), True, False)
+        if t:
+            mm(c("pa", 128, 256), c("ih"), c("c77", 128 * (t - 1), 128 * t), False, False)
+
+    def h_data():
+        mm(c("pa", 0, 128), c("sh"), c("o"), False, False)
+        mm(c("pa", 128, 256), c("i37"), c("o"), False, True)
+
+    def empties():
+        ts(c("emp"), c("o"), 256.0, -8192.0, ge, mul)
+
+    h_consts(0)
+    h_data()
+
+    def offsets():
+        tt(c("y1"), c("pa", 0, 128), c("n8"), mul)
+        for i in (0, 1):
+            q, a = 64 * i, 128 * i
+            tt(c("hz", a, a + 64), c("y1", q, q + 64), c("pa", 128 + q, 192 + q), add)
+            tt(c("hz", a + 64, a + 128), c("y1", 64 - q, 128 - q), c("pa", 128 + q, 192 + q), add)
+            ts(c("hm13", a, a + 128), c("hz", a, a + 128), 8191, None, OP.bitwise_and)
+            cp(c("hu", a, a + 128), c("hm13", a, a + 128))
+
+    def setup_b():
+        ts(c("qa"), c("qsi"), 15, None, OP.bitwise_and)
+        ts(c("hm13"), c("qsi"), 4, None, OP.arith_shift_right)
+        ts(c("qi"), c("qsi"), 2048.0, 1920.0, ge, mul)
+        ts(c("qa"), c("qa"), 128.0, None, mul)
+        tt(c("hm13"), c("hm13"), c("qi"), add)
+        tt(c("qi"), c("qa"), c("hm13"), add)
+        cp(c("ql"), c("qi"))
+        ts(BC, KC, -256.0, 2048.0, mul, add)
+        ts(KX, KC, 16.0, None, mul)
+        ts(WX, WX, 3.0 ** 38, None, mul)
+        cp(TH, c("thi"))
+        cp(c("gc", 0, 8), c("gmb", 0, 128, 16))
+        ts(c("ngc", 0, 8), c("gc", 0, 8), -1.0, None, mul)
+        ts(c("ctb", 0, 128), c("cI"), 32.0, 32.0, ge, mul)
+        ts(c("ctb", 128, 256), c("cI"), 64.0, 32.0, ge, mul)
+        fill(c("on"), 1.0)
+        fill(c("rho"), (7 - rank) / 2048.0)
+        ts(c("bsel", 0, 256), c("bv"), 0.0, None, eq)
+        cp(c("bsel", 256, 512), c("bv"))
+        ts(c("clist"), c("cI", 0, 16), 0.0, None, add)
+        ts(c("sc"), c("cI"), 32.0, -4096.0, ge, mul)
+        ts(c("sc", 64, 128), c("sc", 0, 64), 1.0, None, mul)
+        for t in range(3):
+            ts(c("hm", 128 * t, 128 * t + 128), c("c8"), float(t), c("R", 0, 1), eq, mul)
+
+    def setup_s():
+        for k in range(16):
+            act(k_("bkb", k), c("gmb"), AF.Copy, 0.0, c("R", k, k + 1))
+        for b in (0, 1):
+            w, r = c("pmx", 256 * b, 256 * b + 256), c("bs8", 256 * b, 256 * b + 256)
+            act(r, c("bsel", 256 * b, 256 * b + 256), AF.Copy, 0.0, -8192.0)
+            run("G", lambda: g.affine_select(ap(w), ap(r), [[-1, 16], [0, 2], [-16, 8]], eq, 0.0, 0, 1), [r], [w])
+        act(THR, TH, AF.Identity, -2048.5, -1.0)
+        act(c("gth", 0, 8), c("gc", 0, 8), AF.Copy, 0.0, TH)
+        act(c("of32"), c("cI"), AF.Identity, 0.0625, 0.0)
+        act(c("wi", 0, 8), c("gc", 0, 8), AF.Copy, 0.0, KX)
+        mm(c("pq", 0, 8), c("of32"), c("gth", 0, 8), True, True)
+        mm(c("pq", 8, 16), c("of32"), c("gth", 0, 8), True, True)
+        mm(c("pq", 16, 24), c("wn", 0, 128), c("wi", 0, 8), True, True)
+        mm(c("pq", 24, 32), c("wn", 128, 256), c("wi", 0, 8), True, True)
+        act(c("thc"), c("pq", 0, 16), AF.Identity, 0.75 - (7 - rank) / 16.0)
+        act(c("wsc"), c("pq", 16, 32), AF.Identity, -1.21875)
+        act(c("cht"), c("ch"), AF.Identity, 38.185 * LN3, L3)
+        act(c("ivb"), c("cI"), AF.Copy)
+        act(c("cneg"), c("cI"), AF.Identity, -10240.0, 0.0)
+        act(c("c16"), c("ck"), AF.Identity, 32768.0, -4096.0)
+        act(c("k2"), c("cI"), AF.Identity, 2048.0, 0.0)
+        act(c("c77", 0, 128), c("cI"), AF.Identity, 77.0, 0.0)
+        act(c("c77", 128, 256), c("cI"), AF.Identity, 154.0, 0.0)
+        act(c("fw", 2048, 2064), c("dw", 2048, 2064), AF.Relu, BC)
+        act(c("qlm"), c("gmb"), AF.Copy, 0.0, 128.0)
+        act(c("lenm"), c("gmb"), AF.Copy, 0.0, -256.0)
+        act(c("in8"), c("ihb"), AF.Copy, 0.0, -8192.0)
+        act(c("i8"), c("ihb"), AF.Copy, 0.0, 8192.0)
+        act(c("trit"), c("tri"), AF.Copy, 0.0, 128.0)
+
+    def setup_c():
+        ts(c("stmp"), c("tri"), 256.0, None, mul)
+        tt(c("trie"), c("stmp"), c("i8"), add)
+        ts(c("cst", 0, 128), c("cI"), 2048.0, None, sub)
+        ts(c("cst", 128, 256), c("cI"), 2048.0, None, sub)
+        ts(c("cst", 256, 384), c("ck"), 256.0, 256.0, mul, add)
+        ts(c("dm", 0, 128), c("ck"), KC, None, eq)
+        ts(c("dm", 128, 256), c("ck"), KC, None, eq)
+        ts(c("wts", 0, 2), c("cI", 0, 2), W64, WX, eq, mul)
+
+    def setup_d():
+        ts(c("stmp"), c("tri"), 2.0, None, mul)
+        tt(c("trf"), c("stmp"), c("ih"), sub)
+
+    def setup_f():
+        ts(c("csl", 0, 128), c("cI"), 16.0, -2048.0, mul, add)
+        ts(c("csl", 128, 256), c("cI"), 16.0, -2048.0, mul, add)
+        ts(c("csl", 256, 384), c("ck"), 256.0, 256.0, mul, add)
+        ts(c("lv"), c("cI"), 16.0, -2032.0, mul, add)
+        ts(PP, PC, 64.0, 4096.0, ge, mul)
+        ts(c("k2l"), c("cI"), 0.0, PP, mul, add)
+        ts(c("k2l"), c("k2l"), 2048.0, None, sub)
+
+    def spread(src, k0, k1):
+        for k in range(k0, k1):
+            mm(c("r%d" % (k // 4), 128 * (k % 4), 128 * (k % 4) + 128), k_("bkb", k), c(src), True, True)
+
+    def thermo(e, dst, i):
+        if e == "V":
+            ts(c(dst, 512 * i, 512 * i + 512), c("r%d" % i), BC, 0.0, add, mx)
+        else:
+            act(c(dst, 512 * i, 512 * i + 512), c("r%d" % i), AF.Relu, BC)
+
+    def pick(e, z, a, b, win, off):
+        if e == "V":
+            ts(c(z, a, b), ind(win, off), -1.0, -256.0, mul, mx)
+        else:
+            act(c(z, a, b), ind(win, off), AF.Relu, 256.0, -1.0)
+
+    def slots_gather(e, i):
+        pick(e, "zf", 1024 * i, 1024 * i + 1024, c("fw"), c("ql", 64 * i, 64 * i + 64))
+
+    HB = ("pa", "pq")
+
+    def slots_sum(h, fin):
+        mm(c(HB[h], 0, 128), c("ih"), c("k2l" if fin else "k2"), True, False)
+        for j in range(16):
+            mm(c(HB[h], j, 128, 16), c("zf", 2048 * h + j, 2048 * h + 2048, 16), c("ngc", 0, 8), False, j == 15)
+
+    def slots_turn(h, fin, between=None):
+        q = c("qt", 128 * h, 128 * h + 128)
+        cp(q, c(HB[h], 0, 128))
+        if fin:
+            mm(c(HB[h], 128, 256), c("ih"), c("k2"), True, False)
+        mm(c(HB[h], 128, 256), q, c("ih"), not fin, True)
+        e = c("em", 128 * h, 128 * h + 128)
+        ts(e, c(HB[h], 128, 256), 2048.0 if fin else 0.0, None, eq)
+        if between:
+            between()
+        mm(c(HB[h], 256, 384), c("trf"), e, True, True)
+
+    def slots_put(h, fin):
+        a, b = 128 * h, 128 * h + 128
+        ts(c("fe", a, b), c(HB[h], 256, 384), 0.0, None, lt)
+        tt(c("wmk", a, b), c("fe", a, b), c("npl", a, b), mul)
+        tt(c("yqs" if fin else "qi", a, b), c(HB[h], 128, 256), c("wmk", a, b), add if fin else sub)
+        if not fin:
+            ts(c("ql", a, b), c("qi", a, b), 2048.0, None, add)
+
+    def list_queues():
+        mm(c("pq", 128, 256), c("apb"), c("ih"), True, True)
+        tt(c("ub"), ind(c("ui"), c("clist")), c("dm"), mul)
+        for b in (0, 1):
+            mm(c("pq", 64 + 8 * b, 72 + 8 * b), c("ub", 128 * b, 128 * b + 128), c("gc", 0, 8), True, True)
+
+    def applied():
+        cp(c("qp"), c("pq", 128, 256))
+        cp(c("ul"), c("pq", 64, 80))
+
+    def appended():
+        tt(c("wmk"), ind(c("qp"), c("ul")), c("ipm"), eq)
+        tt(c("npl"), ind(c("qlw"), c("ul")), c("wmk"), mul)
+
+    off = [d for d in T.cores if d != core and topo.chip(d) != topo.chip(core)]
+    near = [d for d in T.cores if d != core and topo.chip(d) == topo.chip(core)]
+    off_e = sorted(set(e for d in off for e in topo.engines(core, d)))
+    near_e = [e for d in near for e in topo.engines(core, d) if e not in off_e]
+
+    def did(d):
+        a = topo.addr(d)
+        return DstId(rid=a[0], pnc=a[1])
+
+    def sums(b, a, z0, stop=True):
+        for k in range(16):
+            mm(c(b, a, a + 64), k_("lkb", k), c("mn", z0 + k, z0 + 1024, 16), False, stop and k == 15)
+
+    for t in range(3):
+        last = t == 2
+        land = "land%d" % t
+        for i in (0, 1):
+            act(c("wg", 1024 * i, 1024 * i + 1024), ind(c("wn"), c("ol", 64 * i, 64 * i + 64)), AF.Copy)
+        if t == 0:
+            offsets()
+            empties()
+            cp(c("ihb"), c("ih"))
+            ts(c("stmp"), c("cI"), PC, None, gt)
+            tt(c("tri"), c("stmp"), c("gmb"), mul)
+            setup_b()
+            setup_s()
+        else:
+            for i in range(4):
+                thermo("S", "fw", i)
+            for i in range(4):
+                slots_gather("S", i)
+        mm(c("plo", 0, 128), c("ih"), c("pre"), True, False)
+        mm(c("plo", 64, 128), c("ih"), c("emp", 0, 64), False, False)
+        mm(c("phi", 0, 64), c("ih"), c("pre", 0, 64), True, False)
+
+        def records(i, other):
+            a = 2048 * i + 1024 * other
+            tt(c("mn", a, a + 1024), ind(c("xs"), c("hu", 128 * i + 64 * other, 128 * i + 64 * other + 64)),
+               c("wg", 1024 * i, 1024 * i + 1024), mi)
+            return a
+
+        sums("plo", 0, records(0, 0), False)
+        if t:
+            list_queues()
+        sums("plo", 64, records(0, 1))
+        mm(c("r3", 0, 64), c("ih"), c("emp", 64, 128), True, False)
+        mm(c("r3", 0, 64), c("ih"), c("pre", 0, 64), False, False)
+        sums("phi", 0, records(1, 0))
+        if t == 1:
+            setup_f()
+        cp(c("ml"), c("plo", 0, 64))
+        tt(c("dlo"), c("plo", 64, 128), c("ml"), sub)
+        sums("r3", 0, records(1, 1))
+        if t:
+            applied()
+            appended()
+            slots_sum(0, False)
+        cp(c("sd", 64, 128), c("phi", 0, 64))
+        tt(c("dhi"), c("r3", 0, 64), c("sd", 64, 128), sub)
+        tt(c("dd"), c("dhi"), c("dlo"), add)
+        ts(c("s"), c("dd"), 0.0, None, gt)
+        tt(c("dlo"), c("s"), c("dlo"), mul)
+        tt(c("dhi"), c("s"), c("dhi"), mul)
+        tt(c("cp", 0, 64), c("ml"), c("dlo"), add)
+        tt(c("cp", 64, 128), c("phi", 0, 64), c("dhi"), add)
+        spread("cp", 0, 4)
+        if t:
+            slots_turn(0, False, lambda: spread("cp", 4, 8))
+        else:
+            spread("cp", 4, 8)
+        spread("cp", 8, 16)
+        thermo("V", "dw", 0)
+        if t:
+            slots_put(0, False)
+        thermo("V", "dw", 2)
+        thermo("S", "dw", 1)
+        thermo("S", "dw", 3)
+        if t:
+            slots_sum(1, False)
+        for b in (0, 1):
+            mm(c("plo", 0, 256), c("ctb", 128 * b, 128 * b + 128), c("bsel", 256 * b, 256 * b + 256), b == 0, False)
+        mm(c("plo", 0, 256), c("on"), c("rho"), False, False)
+        for b in (0, 1):
+            m = (32, 64)[b]
+            z = 2048 * b
+            pick("V", "zd", z, z + 16 * m, c("dw"), c("ql", 128 * b, 128 * b + m))
+            pick("S", "zd", z + 16 * m, z + 2048, c("dw"), c("ql", 128 * b + m, 128 * b + 128))
+            if b == 0 and t:
+                slots_turn(1, False)
+                slots_put(1, False)
+            for j in range(16):
+                mm(c("plo", 16 * j + 8 * b, 16 * j + 8 * b + 8), c("zd", z + j, z + 2048, 16), c("ngc", 0, 8), False, b == 1 and j == 15)
+        own = c(land, 16 * rank, 16 * rank + 16)
+        cp(c("tsb", 128, 256), c("plo", 128, 256))
+        tt(c("tm", 0, 128), c("plo", 0, 128), c("tsb", 128, 256), mx)
+        tt(c("tm", 128, 192), c("tm", 0, 64), c("tm", 64, 128), mx)
+        tt(c("tm", 192, 224), c("tm", 128, 160), c("tm", 160, 192), mx)
+        tt(own, c("tm", 192, 208), c("tm", 208, 224), mx)
+        for a in hist[land]:
+            wait("G", a[3])
+        src = T[land][:, 16 * rank:16 * rank + 16]
+        sem = T.sem["arr%d" % t]
+        moves = [RemoteDMATransfer(dst_ids=[did(d) for d in off], dma_engine_mask=sum(1 << e for e in off_e), remote_sem=sem,
+                                   srcs=[src], dsts=[src for d in off])]
+        if near:
+            moves.append(RemoteDMATransfer(dst_ids=[did(d) for d in near], dma_engine_mask=sum(1 << e for e in near_e),
+                                           remote_sem=sem, srcs=[src], dsts=[src for d in near]))
+        g.remote_dma_fused(moves, local_sem=T.sem.loc)
+        arrive = len(off_e) * len(off) + len(near_e) * len(near)
+        if t == 0:
+            setup_c()
+        cp(c("tsb", 0, 128), c("plo", 0, 128))
+        tt(c("x2", 0, 64), c("o", 64, 128), c("o", 0, 64), sub)
+        tt(c("x2", 64, 128), c("cp", 64, 128), c("cp", 0, 64), sub)
+        ts(c("qa"), c("qi"), 3975, None, OP.bitwise_and)
+        tt(c("x2", 128, 192), c("x2", 0, 64), c("s"), mul)
+        tt(c("x2", 192, 256), c("x2", 64, 128), c("s"), mul)
+        ts(c("hfs"), c("qa"), float(t + (2048 if t else 0)), None, eq)
+        tt(c("o2", 0, 64), c("o", 0, 64), c("x2", 128, 192), add)
+        tt(c("o2", 64, 128), c("o", 64, 128), c("x2", 128, 192), sub)
+        tt(c("c2", 0, 64), c("cp", 0, 64), c("x2", 192, 256), add)
+        tt(c("c2", 64, 128), c("cp", 64, 128), c("x2", 192, 256), sub)
+        cp(c("ol2"), c("o2"))
+        for b in (0, 1):
+            mm(c("phi", 0, 256), c("hfs", 128 * b, 128 * b + 128), c("pmx", 256 * b, 256 * b + 256), b == 0, b == 1)
+        mm(c("plo", 0, 128), c("ih"), c("c2"), True, False)
+        mm(c("plo", 0, 128), c("ih"), c("emp"), False, False)
+        mm(c("plo", 0, 128), c("in8"), c("hm", 128 * t, 128 * t + 128), False, False)
+        mm(c("plo", 0, 128), c("ih"), c("sc"), False, False)
+        ts(c("p16", 32, 48), own, 1.0, -100.0, lt, mul)
+        tt(c("ce", 0, 256), c("phi", 0, 256), c("tsb"), add)
+        tt(c("p16", 64, 80), own, c("p16", 32, 48), add)
+        tt(c("ce", 256, 384), c("ce", 0, 128), c("ce", 128, 256), mi)
+        tt(c("ce", 384, 448), c("ce", 256, 320), c("ce", 320, 384), mi)
+        tt(c("ce", 448, 480), c("ce", 384, 416), c("ce", 416, 448), mi)
+        tt(c("p16", 0, 16), c("ce", 448, 464), c("ce", 464, 480), mi)
+        ts(c("p16", 16, 32), c("p16", 0, 16), 1.0, -20000.0, lt, mul)
+        tt(c("p16", 48, 64), c("p16", 0, 16), c("thc"), add)
+        tt(c("p16", 80, 96), c("p16", 48, 64), c("p16", 16, 32), add)
+        mm(c("phi", 0, 384), c("ih"), c("csl" if last else "cst"), True, False)
+        mm(c("r0", 0, 128), c("ih"), c("cneg"), True, False)
+        mm(c("r0", 0, 128), c("ih"), c("o2"), False, False)
+        if t == 0:
+            setup_d()
+        g.vector.wait_ge(sem, arrive)
+        tt(c("kt", 0, 64), c(land, 0, 64), c(land, 64, 128), mx)
+        tt(c("kt", 64, 96), c("kt", 0, 32), c("kt", 32, 64), mx)
+        tt(c("kp"), c("kt", 64, 80), c("kt", 80, 96), mx)
+        ts(c("kb"), ind(c("kp"), c("clist")), -2048.21875, None, add)
+        for b in (0, 1):
+            mm(c("pa", 128 * b, 128 * b + 128), c("kb", 128 * b, 128 * b + 128), c("ih"), True, True)
+        tt(c("zi"), c("kp"), c("wsc"), add)
+        tt(c("p16", 96, 112), c("kp"), c("p16", 64, 80), eq)
+        tt(c("p16", 112, 128), c("kp"), c("p16", 80, 96), gt)
+        ts(c("ui"), c("zi"), 127, None, OP.bitwise_and)
+        ts(c("wm", 0, 256), c("pa", 0, 256), BC, 0.0, add, mx)
+        for i in (0, 1):
+            pick("V", "ze", 1024 * i, 1024 * i + 512, c("wm"), c("ol2", 64 * i, 64 * i + 32))
+            pick("S", "ze", 1024 * i + 512, 1024 * i + 1024, c("wm"), c("ol2", 64 * i + 32, 64 * i + 64))
+            for k in range(16):
+                mm(c("plo", 64 * i, 64 * i + 64), k_("lkb", k), c("ze", 1024 * i + k, 1024 * i + 1024, 16), False, i == 1 and k == 15)
+        tt(c("p16", 128, 144), c("p16", 96, 112), c("p16", 112, 128), mul)
+        ts(c("p16", 128, 144), c("p16", 128, 144), -200.0, 200.0, mul, add)
+        tt(c("p16", 144, 160), c("ui"), c("p16", 128, 144), add)
+        for i in range(16):
+            ts(k_("oh", i), c("ivb"), c("p16", 144 + i, 145 + i), None, eq)
+        ts(c("st"), c("plo", 0, 128), THR, None, ge)
+        mm(c("r0", 0, 128), c("trie"), c("st"), False, True)
+        mm(c("phi", 0, 128), c("tri" if last else "trit"), c("st"), False, False)
+        mm(c("phi", 128, 256), c("gmb" if last else "qlm"), c("st"), False, False)
+        mm(c("phi", 256, 384), c("st"), c("lenm"), False, True)
+        mm(c("plo", 0, 128), c("ih"), c("c16"), True, False)
+        for i in range(16):
+            b, h = i // 8, i % 8
+            mm(c("pq", 4 * h + 2 * b, 4 * h + 2 * b + 2), k_("oh", i), c("wts", 0, 2), True, True)
+        act(c("lna", 0, 32), c("pq", 0, 32), AF.Ln, 2.0 ** -63)
+        cp(c("e16"), c("r0", 0, 128))
+
+        def follow():
+            tt(c("tt"), c("phi", 0, 128), c("st"), mul)
+            tt(c("x2", 0, 64), c("tt", 64, 128), c("tt", 0, 64), sub)
+            tt(c("x2", 64, 128), c("x2", 0, 64), c("s"), mul)
+            tt(c("tof", 0, 64), c("tt", 0, 64), c("x2", 64, 128), add)
+            tt(c("tof", 64, 128), c("tt", 64, 128), c("x2", 64, 128), sub)
+
+        if last:
+            follow()
+            spread("tof", 0, 16)
+        for r in range(16):
+            ts(k_("fr", r), c("e16"), 256.0 * r - 2048.0, 256.0 * r - 1792.0, mx, mi)
+            mm(c("plo", r, 128, 16), k_("fr", r), c("gc", 0, 8), False, r == 15)
+        if not last:
+            follow()
+        ts(c("lna", 32, 64), c("lna", 0, 32), -35.0, 1000.0, lt, mul)
+        tt(c("lna", 64, 96), c("cht"), c("lna", 0, 32), sub)
+        ts(c("corr"), c("phi", 256, 384), 256.0, None, mi)
+        tt(c("lna", 96, 128), c("lna", 64, 96), c("lna", 32, 64), add)
+        ts(c("iseq"), c("phi", 256, 384), 256.0, None, eq)
+        tt(c("lna", 128, 144), c("lna", 96, 128, 2), c("lna", 97, 128, 2), mi)
+        if last:
+            tt(c("l16"), c("phi", 128, 256), c("lv"), lt)
+        else:
+            act(c("qlw"), c("phi", 128, 256), AF.Relu, 0.0, -1.0)
+        tt(c("lna", 144, 152), c("lna", 128, 144, 2), c("lna", 129, 144, 2), mi)
+        if last:
+            tt(c("qlw"), c("phi", 128, 256), c("l16"), mul)
+        ts(c("lna", 152, 160), c("lna", 144, 152), 1.0 / LN3, 256.0, mul, mi)
+        ts(c("apf"), c("lna", 152, 160), 12582912.0, 12583168.0, add, sub)
+        tt(c("appl"), ind(c("apf"), c("clist", 0, 8)), c("iseq"), mul)
+        tt(c("corr"), c("corr"), c("appl"), add)
+        act(c("apb"), ind(c("apf"), c("clist", 0, 8)), AF.Copy)
+        tt(c("o3t"), c("plo", 0, 128), c("corr"), add)
+        mm(c("plo", 128, 256), c("o3t"), c("ih"), True, True)
+        if not last:
+            h_consts(t + 1)
+            cp(c("o"), c("plo", 128, 256))
+            cp(c("ol"), c("plo", 128, 256))
+            h_data()
+            spread("tof", 0, 16)
+            offsets()
+            empties()
+        else:
+            cp(c("yo"), c("plo", 128, 256))
+            run("Y", lambda: g.sync.dma_start(T.yoc[:, :], T.yo[:, :]), [c("yo")], [], sem="d_yo", inc=16)
+            list_queues()
+            for i in range(4):
+                thermo("VS"[i & 1], "fw", i)
+            applied()
+            appended()
+            for h in (0, 1):
+                slots_gather("V", 2 * h)
+                slots_gather("S", 2 * h + 1)
+                slots_sum(h, True)
+            for h in (0, 1):
+                slots_turn(h, True)
+                slots_put(h, True)
+            run("Y", lambda: g.sync.dma_start(T.yq[:, :], T.yqs[:, :]), [c("yqs")], [], sem="d_yq", inc=16)
+    g.sync.wait_ge(T.sem.d_yo, 16)
+    g.sync.wait_ge(T.sem.d_yq, 16)
+    for e in ("V", "S", "P", "G"):
+        g.wait_ge(T.sem["c" + e], count[e])
+    g.wait_ge(T.sem.loc, 3 * (len(off_e) + (len(near_e) if near else 0)))

@@ -34,6 +34,78 @@ PART = {"pint": ("cint", 0, 1), "kint": ("cint", 1, 1), "gint": ("cint", 2, 1), 
         "thc": ("pc", 16, 16), "wsc": ("pc", 32, 16), "zi": ("zu", 0, 16), "ui": ("zu", 16, 16)}
 
 
+CYCLE, WAKE, TRIP, SLACK = 1.0, 90.0, 5000.0, 5.0
+PLAN = {}
+
+
+def plan(ops, trips):
+    n = len(ops)
+    pred = [dict() for _ in range(n)]
+    hist, bank = {}, {}
+    for i, op in enumerate(ops):
+        e = op[0]
+        regs = [(False, rg[0], rg[1], rg[2]) for rg in op[2]] + [(True, rg[0], rg[1], rg[2]) for rg in op[3]]
+        for wr, b, lo, hi in regs:
+            if b in PSUM:
+                for k, v in bank.get(b, {}).items():
+                    pred[i][v] = max(pred[i].get(v, 0), int(k != e))
+            else:
+                for a in hist.get(b, []):
+                    if a[1] < hi and lo < a[2] and (wr or a[0]):
+                        pred[i][a[3]] = 1
+        for wr, b, lo, hi in regs:
+            if b in PSUM:
+                bank.setdefault(b, {})[e] = i
+            else:
+                h = hist.setdefault(b, [])
+                if wr:
+                    h[:] = [a for a in h if not (lo <= a[1] and a[2] <= hi)]
+                h.append((wr, lo, hi, i))
+    for a, b in trips:
+        pred[b][a] = 2
+    succ = [[] for _ in range(n)]
+    for i in range(n):
+        for p, k in pred[i].items():
+            succ[p].append((i, k))
+    way = [0.0] * n
+    for i in range(n - 1, -1, -1):
+        way[i] = ops[i][6] + max([way[j] + (0, WAKE, TRIP)[k] for j, k in succ[i]] or [0.0])
+    left = [len(p) for p in pred]
+    ready = {e: [i for i in range(n) if ops[i][0] == e and not left[i]] for e in "VSPGY"}
+    free, newest, end, order = dict.fromkeys("VSPGY", 0.0), dict.fromkeys("VSPGY", -1), [0.0] * n, []
+
+    def begin(i):
+        e = ops[i][0]
+        t = free[e]
+        for p, k in pred[i].items():
+            if k == 2:
+                t = max(t, end[p] + TRIP)
+            elif k == 1 and (end[p] > free[e] or newest[e] == p):
+                t = max(t, end[p] + WAKE)
+        return t
+
+    while len(order) < n:
+        best = None
+        for e in "VSPGY":
+            if ready[e]:
+                st = [(begin(i), i) for i in ready[e]]
+                t0 = min(st)[0]
+                t, i = max(((t, i) for t, i in st if t <= t0 + SLACK), key=lambda q: (way[q[1]] - q[0], -q[1]))
+                if best is None or t < best[0]:
+                    best = (t, i, e)
+        t, i, e = best
+        ready[e].remove(i)
+        end[i] = t + ops[i][6]
+        free[e] = t + 70 if e == "Y" else end[i]
+        newest[e] = i
+        order.append(i)
+        for j, k in succ[i]:
+            left[j] -= 1
+            if not left[j]:
+                ready[ops[j][0]].append(j)
+    return order
+
+
 def rank_program(g, core, T, topo):
     rank = T.rank_of(core)
     if rank is None:
@@ -42,6 +114,8 @@ def rank_program(g, core, T, topo):
     count = {"V": 0, "S": 0, "P": 0, "G": 0}
     known = {e: {} for e in eng}
     snap = {}
+    ops = []
+    trips = []
     hist = {}
     bank = {}
 
@@ -53,7 +127,10 @@ def rank_program(g, core, T, topo):
             if known[e].get(k, 0) < v:
                 known[e][k] = v
 
-    def run(e, fn, reads, writes, sem=None, inc=1):
+    def run(e, fn, reads, writes, sem=None, inc=1, cost=100.0, pre=None):
+        ops.append((e, fn, reads, writes, sem, inc, cost, pre))
+
+    def emit(e, fn, reads, writes, sem, inc, cost, pre):
         evs = []
         for wr, regs in ((False, reads), (True, writes)):
             for rg in regs:
@@ -67,6 +144,11 @@ def rank_program(g, core, T, topo):
             need[k] = max(need.get(k, 0), v)
         for ev in sorted(need.items(), key=lambda q: -q[1]):
             wait(e, ev)
+        if pre:
+            pre()
+        if not inc:
+            fn()
+            return
         if sem is None:
             sem = "c" + e
             count[e] += 1
@@ -87,7 +169,6 @@ def rank_program(g, core, T, topo):
                     else:
                         h[:] = [a for a in h if not (not a[0] and a[3][0] == ev[0] and a[1] == lo and a[2] == hi)]
                     h.append((wr, lo, hi, ev))
-        return ev
 
     def c(b, lo=None, hi=None, step=1):
         n, at, w = PART.get(b) or (b, 0, SCRATCH[b][1][1])
@@ -113,36 +194,49 @@ def rank_program(g, core, T, topo):
     def val(x):
         return ap(x) if isinstance(x, tuple) else x
 
+    def wide(x):
+        return 16 * (x[2][2] - x[2][1]) if x[0] == "ind" else -(-(x[2] - x[1]) // x[3])
+
+    def took(out, *ins):
+        if any(x[0] == "ind" for x in ins):
+            return 50 + 1.56 * CYCLE * wide(out)
+        small = all(SCRATCH[x[0]][2] in (BF, H, U16) for x in (out,) + ins)
+        both = len(ins) == 2 and not any(x[0] in PSUM for x in ins)
+        return CYCLE * max(64, wide(out) * (2 if both else 0.5 if small and len(ins) == 1 else 1))
+
     def ts(out, a, s1, s2, o0, o1=None):
         if o1 is None:
-            run("V", lambda: g.vector.tensor_scalar(ap(out), ap(a), val(s1), None, o0), rd(a, s1), [out])
+            run("V", lambda: g.vector.tensor_scalar(ap(out), ap(a), val(s1), None, o0), rd(a, s1), [out], cost=took(out, a))
         else:
-            run("V", lambda: g.vector.tensor_scalar(ap(out), ap(a), val(s1), val(s2), o0, o1), rd(a, s1, s2), [out])
+            run("V", lambda: g.vector.tensor_scalar(ap(out), ap(a), val(s1), val(s2), o0, o1), rd(a, s1, s2), [out], cost=took(out, a))
 
     def tt(out, a, b, op):
-        run("V", lambda: g.vector.tensor_tensor(ap(out), ap(a), ap(b), op), rd(a, b), [out])
+        run("V", lambda: g.vector.tensor_tensor(ap(out), ap(a), ap(b), op), rd(a, b), [out], cost=took(out, a, b))
 
     def cp(out, a):
-        run("V", lambda: g.vector.tensor_copy(ap(out), ap(a)), rd(a), [out])
+        run("V", lambda: g.vector.tensor_copy(ap(out), ap(a)), rd(a), [out], cost=took(out, a))
 
     def fill(out, v):
-        run("V", lambda: g.vector.memset(ap(out), v), [], [out])
+        run("V", lambda: g.vector.memset(ap(out), v), [], [out], cost=took(out))
 
     def act(out, a, func, bias=0.0, scale=1.0):
-        run("S", lambda: g.scalar.activation(ap(out), ap(a), func, bias=val(bias), scale=val(scale)), rd(a, bias, scale), [out])
+        cost = 65 + 1.56 * CYCLE * wide(out) if a[0] == "ind" else CYCLE * max(64, wide(out))
+        run("S", lambda: g.scalar.activation(ap(out), ap(a), func, bias=val(bias), scale=val(scale)), rd(a, bias, scale), [out],
+            cost=cost + (1300 if func == AF.Exp else 0))
 
     def mm(out, l, r, start, stop):
-        run("P", lambda: g.tensor.matmul(ap(out), ap(l), ap(r), start, stop), rd(l, r), [out])
+        run("P", lambda: g.tensor.matmul(ap(out), ap(l), ap(r), start, stop), rd(l, r), [out],
+            cost=CYCLE * max(min(64, wide(l)), wide(r)) * (4 if SCRATCH[l[0]][2] == F32 else 1))
 
     def iota(out, pattern, base, cm):
-        small = SCRATCH[out[0]][2] != I32
-        if small:
-            run("G", lambda: g.iota(ap(out), pattern, base, cm, allow_small_or_imprecise_dtypes=True), [], [out])
+        cost = 130 + 2 * CYCLE * wide(out)
+        if SCRATCH[out[0]][2] != I32:
+            run("G", lambda: g.iota(ap(out), pattern, base, cm, allow_small_or_imprecise_dtypes=True), [], [out], cost=cost)
         else:
-            run("G", lambda: g.iota(ap(out), pattern, base, cm), [], [out])
+            run("G", lambda: g.iota(ap(out), pattern, base, cm), [], [out], cost=cost)
 
     def load(e, sem, b, hi, src):
-        run(e, lambda: eng[e].dma_start(T[b][:, 0:hi], src), [], [c(b, 0, hi)], sem=sem, inc=16)
+        run(e, lambda: eng[e].dma_start(T[b][:, 0:hi], src), [], [c(b, 0, hi)], sem=sem, inc=16, cost=9000.0 if b == "xs" else 2000.0)
 
     def k_(b, k):
         return c(b, 128 * k, 128 * k + 128)
@@ -253,7 +347,7 @@ def rank_program(g, core, T, topo):
         for b in (0, 1):
             w, r = c("pmx", 256 * b, 256 * b + 256), c("bs8", 256 * b, 256 * b + 256)
             act(r, c("bsel", 256 * b, 256 * b + 256), AF.Copy, 0.0, -8192.0)
-            run("G", lambda: g.affine_select(ap(w), ap(r), [[-1, 16], [0, 2], [-16, 8]], eq, 0.0, 0, 1), [r], [w])
+            run("G", lambda w=w, r=r: g.affine_select(ap(w), ap(r), [[-1, 16], [0, 2], [-16, 8]], eq, 0.0, 0, 1), [r], [w], cost=600.0)
         act(THR, TH, AF.Identity, -2048.5, -1.0)
         act(c("gth", 0, 8), c("gc", 0, 8), AF.Copy, 0.0, TH)
         act(c("of32"), c("cI"), AF.Identity, 0.0625, 0.0)
@@ -459,8 +553,6 @@ def rank_program(g, core, T, topo):
         tt(c("tm", 128, 192), c("tm", 0, 64), c("tm", 64, 128), mx)
         tt(c("tm", 192, 224), c("tm", 128, 160), c("tm", 160, 192), mx)
         tt(own, c("tm", 192, 208), c("tm", 208, 224), mx)
-        for a in hist[land]:
-            wait("G", a[3])
         src = T[land][:, 16 * rank:16 * rank + 16]
         sem = T.sem["arr%d" % t]
         moves = [RemoteDMATransfer(dst_ids=[did(d) for d in off], dma_engine_mask=sum(1 << e for e in off_e), remote_sem=sem,
@@ -468,7 +560,8 @@ def rank_program(g, core, T, topo):
         if near:
             moves.append(RemoteDMATransfer(dst_ids=[did(d) for d in near], dma_engine_mask=sum(1 << e for e in near_e),
                                            remote_sem=sem, srcs=[src], dsts=[src for d in near]))
-        g.remote_dma_fused(moves, local_sem=T.sem.loc)
+        run("G", lambda moves=moves: g.remote_dma_fused(moves, local_sem=T.sem.loc), [own], [], inc=0, cost=300.0)
+        sent = len(ops) - 1
         arrive = len(off_e) * len(off) + len(near_e) * len(near)
         if t == 0:
             setup_c()
@@ -505,8 +598,9 @@ def rank_program(g, core, T, topo):
         mm(c("r0", 0, 128), c("ih"), c("o2"), False, False)
         if t == 0:
             setup_d()
-        g.vector.wait_ge(sem, arrive)
         tt(c("kt", 0, 64), c(land, 0, 64), c(land, 64, 128), mx)
+        ops[-1] = ops[-1][:7] + (lambda sem=sem, n=arrive: g.vector.wait_ge(sem, n),)
+        trips.append((sent, len(ops) - 1))
         tt(c("kt", 64, 96), c("kt", 0, 32), c("kt", 32, 64), mx)
         tt(c("kp"), c("kt", 64, 80), c("kt", 80, 96), mx)
         ts(c("kb"), ind(c("kp"), c("clist")), -2048.21875, None, add)
@@ -598,6 +692,10 @@ def rank_program(g, core, T, topo):
                 slots_turn(h, True)
                 slots_put(h, True)
             run("Y", lambda: g.sync.dma_start(T.yq[:, :], T.yqs[:, :]), [c("yqs")], [], sem="d_yq", inc=16)
+    if "order" not in PLAN:
+        PLAN["order"] = plan(ops, trips)
+    for i in PLAN["order"]:
+        emit(*ops[i])
     g.sync.wait_ge(T.sem.d_yo, 16)
     g.sync.wait_ge(T.sem.d_yq, 16)
     for e in ("V", "S", "P", "G"):

@@ -2,7 +2,6 @@ import math
 from concourse.bass import DstId, RemoteDMATransfer
 from concourse.mybir import AluOpType as OP, ActivationFunctionType as AF
 
-LN3 = math.log(3.0)
 F32, BF, H, I32, U16 = "float32", "bfloat16", "float16", "int32", "uint16"
 
 
@@ -12,19 +11,18 @@ def _sb(dtype, **names):
 
 SCRATCH = {}
 SCRATCH.update(_sb(BF, xs=8192, wn=272, gmb=128, lkb=2048, apb=128, bkb=2048, tri=128, i8=128, in8=128, qlm=128, lenm=128,
-                   trit=128, bs8=512, cneg=128, c16=128, k2=128, c77=256, trf=128, ihb=128, sm=64, ctb=256, on=128, rho=256,
-                   bsel=512, pmx=512, dm=256, ivb=128, hm=384, wg=2048, mn=4096, zd=4096, zf=4096, ze=2048, hfs=256,
+                   trit=128, cneg=128, c16=128, k2=128, c77=256, trf=128, ihb=128, sm=64, ctb=256, on=128, rho=256,
+                   dm=256, ivb=128, hm=384, wg=2048, mn=4096, zd=4096, zf=4096, ze=2048, hfs=256,
                    oh=2048, ub=256))
 SCRATCH.update(_sb(I32, oci=128, qsi=256, thi=1, cint=8, qi=256, qa=256, hz=256, hm13=256, zu=32))
 SCRATCH.update(_sb(U16, ol=128, ql=256, hu=256, ol2=128, clist=16, ul=16))
 SCRATCH.update(_sb(H, ih=128, sh=128, stmp=128, hcb=256, i37=128, pre=128, emp=128, sc=128, trie=128, cst=384, csl=384,
                    k2l=128, o=128, cp=128, c2=128, o2=128, kb=256, st=128, e16=128, fr=2048, o3t=128, tof=128, em=256,
                    qt=256))
-SCRATCH.update(_sb(F32, col=32, cI=128, cg=128, ck=128, c8=128, ipm=256, pv=256, bv=256, ch=32, cht=32, R=16, n8=128,
+SCRATCH.update(_sb(F32, col=32, cI=128, cg=128, ck=128, c8=128, ipm=256, rs=256, rb=256, rb4=32, ch=32, cht=32, cno=32, R=16, n8=128,
                    sx=320, pc=48, of32=128, y1=128, sd=128, dw=2064, fw=2064, tsb=256, tm=256, land0=128, land1=128,
                    land2=128, x2=256, ce=512, p16=160, kt=128, kp=16, wm=272, lna=160, apf=8, qp=128, corr=128, iseq=128,
                    appl=128, qlw=128, l16=128, lv=128, tt=128, wmk=256, npl=256, fe=256, yo=128, yqs=256))
-del SCRATCH["pv"]
 PSUM = ("r0", "r1", "r2", "r3", "pa", "plo", "phi", "pq")
 SCRATCH.update({n: ("psum", [128, 512], F32) for n in PSUM})
 SEMAPHORES = ["cV", "cS", "cP", "cG", "d_oc", "d_qs", "d_wn", "d_th", "d_x", "d_yo", "d_yq", "arr0", "arr1", "arr2", "loc"]
@@ -34,7 +32,7 @@ PART = {"pint": ("cint", 0, 1), "kint": ("cint", 1, 1), "gint": ("cint", 2, 1), 
         "thc": ("pc", 16, 16), "wsc": ("pc", 32, 16), "zi": ("zu", 0, 16), "ui": ("zu", 16, 16)}
 
 
-CYCLE, WAKE, TRIP, SLACK = 1.0, 90.0, 5000.0, 5.0
+CYCLE, WAKE, TRIP, SLACK = 1.0, 120.0, 4700.0, 5.0
 PLAN = {}
 
 
@@ -70,40 +68,52 @@ def plan(ops, trips):
     way = [0.0] * n
     for i in range(n - 1, -1, -1):
         way[i] = ops[i][6] + max([way[j] + (0, WAKE, TRIP)[k] for j, k in succ[i]] or [0.0])
-    left = [len(p) for p in pred]
-    ready = {e: [i for i in range(n) if ops[i][0] == e and not left[i]] for e in "VSPGY"}
-    free, newest, end, order = dict.fromkeys("VSPGY", 0.0), dict.fromkeys("VSPGY", -1), [0.0] * n, []
 
-    def begin(i):
-        e = ops[i][0]
-        t = free[e]
-        for p, k in pred[i].items():
-            if k == 2:
-                t = max(t, end[p] + TRIP)
-            elif k == 1 and (end[p] > free[e] or newest[e] == p):
-                t = max(t, end[p] + WAKE)
-        return t
+    def forward(urgent, back):
+        after = succ if not back else [list(p.items()) for p in pred]
+        before = [list(p.items()) for p in pred] if not back else succ
+        left = [len(p) for p in before]
+        ready = {e: [i for i in range(n) if ops[i][0] == e and not left[i]] for e in "VSPGY"}
+        free, newest, end, order = dict.fromkeys("VSPGY", 0.0), dict.fromkeys("VSPGY", -1), [0.0] * n, []
 
-    while len(order) < n:
-        best = None
-        for e in "VSPGY":
-            if ready[e]:
-                st = [(begin(i), i) for i in ready[e]]
-                t0 = min(st)[0]
-                t, i = max(((t, i) for t, i in st if t <= t0 + SLACK), key=lambda q: (way[q[1]] - q[0], -q[1]))
-                if best is None or t < best[0]:
-                    best = (t, i, e)
-        t, i, e = best
-        ready[e].remove(i)
-        end[i] = t + ops[i][6]
-        free[e] = t + 70 if e == "Y" else end[i]
-        newest[e] = i
-        order.append(i)
-        for j, k in succ[i]:
-            left[j] -= 1
-            if not left[j]:
-                ready[ops[j][0]].append(j)
-    return order
+        def begin(i):
+            e = ops[i][0]
+            t = free[e]
+            for p, k in before[i]:
+                if k == 2:
+                    t = max(t, end[p] + TRIP)
+                elif k == 1 and (end[p] > free[e] or newest[e] == p):
+                    t = max(t, end[p] + WAKE)
+            return t
+
+        while len(order) < n:
+            best = None
+            for e in "VSPGY":
+                if ready[e]:
+                    st = [(begin(i), i) for i in ready[e]]
+                    t0 = min(st)[0]
+                    t, i = max(((t, i) for t, i in st if t <= t0 + SLACK), key=lambda q: (urgent[q[1]], q[1] if back else -q[1]))
+                    if best is None or t < best[0]:
+                        best = (t, i, e)
+            t, i, e = best
+            ready[e].remove(i)
+            end[i] = t + ops[i][6]
+            free[e] = t + 70 if e == "Y" and not back else end[i]
+            newest[e] = i
+            order.append(i)
+            for j, k in after[i]:
+                left[j] -= 1
+                if not left[j]:
+                    ready[ops[j][0]].append(j)
+        return max(end), order, end
+
+    best, urgent = None, way
+    for i in range(4):
+        total, order, end = forward(urgent, False)
+        if best is None or total < best[0]:
+            best = (total, order)
+        urgent = forward(end, True)[2]
+    return best[1]
 
 
 def rank_program(g, core, T, topo):
@@ -216,6 +226,9 @@ def rank_program(g, core, T, topo):
     def cp(out, a):
         run("V", lambda: g.vector.tensor_copy(ap(out), ap(a)), rd(a), [out], cost=took(out, a))
 
+    def scan(out, d0, d1, o0, o1):
+        run("V", lambda: g.vector.tensor_tensor_scan(ap(out), ap(d0), ap(d1), 0.0, o0, o1), rd(d0, d1), [out], cost=CYCLE * max(64, wide(out)))
+
     def fill(out, v):
         run("V", lambda: g.vector.memset(ap(out), v), [], [out], cost=took(out))
 
@@ -257,12 +270,11 @@ def rank_program(g, core, T, topo):
     iota(c("ck"), [[0, 8], [1, 16]], 0, 0)
     iota(c("c8"), [[0, 16], [1, 8]], 0, 0)
     iota(c("ch"), [[0, 8], [64, 4]], 0, 0)
-    iota(c("bv"), [[0, 16], [1, 2], [0, 8]], 0, 0)
     iota(c("ipm"), [[1, 256]], -256, 0)
 
     fill(c("wn", 256, 272), 0.0)
     fill(c("lkb"), 0.0)
-    fill(LN, 3.0)
+    fill(LN, math.exp(43.23))
     fill(c("dw", 2048, 2064), 0.0)
     fill(c("wm", 256, 272), 0.0)
     ts(c("kint"), c("pint"), 15, None, OP.bitwise_and)
@@ -285,7 +297,7 @@ def rank_program(g, core, T, topo):
     ts(c("n8"), c("cI"), 2.0, K8, mul, add)
     cp(c("o"), c("oci"))
     cp(c("ol"), c("oci"))
-    act(WX, P64, AF.Exp, 0.0, -LN3)
+    act(WX, P64, AF.Exp, 43.0, -1.0)
     act(L3, LN, AF.Ln)
     for k in range(16):
         act(c("lkb", 128 * k + k, 128 * k + 128, 16), c("gmb", k, 128, 16), AF.Copy)
@@ -325,7 +337,6 @@ def rank_program(g, core, T, topo):
         cp(c("ql"), c("qi"))
         ts(BC, KC, -256.0, 2048.0, mul, add)
         ts(KX, KC, 16.0, None, mul)
-        ts(WX, WX, 3.0 ** 38, None, mul)
         cp(TH, c("thi"))
         cp(c("gc", 0, 8), c("gmb", 0, 128, 16))
         ts(c("ngc", 0, 8), c("gc", 0, 8), -1.0, None, mul)
@@ -333,8 +344,10 @@ def rank_program(g, core, T, topo):
         ts(c("ctb", 128, 256), c("cI"), 64.0, 32.0, ge, mul)
         fill(c("on"), 1.0)
         fill(c("rho"), (7 - rank) / 2048.0)
-        ts(c("bsel", 0, 256), c("bv"), 0.0, None, eq)
-        cp(c("bsel", 256, 512), c("bv"))
+        for b in (0, 1):
+            ts(c("rs", 128 * b, 128 * b + 128), c("ck"), 0.0, None, gt)
+            ts(c("rb", 128 * b, 128 * b + 128), c("ck"), 0.0, 1e5, eq, mul)
+        ts(c("rb4"), c("ch"), 0.0, 1e5, eq, mul)
         ts(c("clist"), c("cI", 0, 16), 0.0, None, add)
         ts(c("sc"), c("cI"), 32.0, -4096.0, ge, mul)
         ts(c("sc", 64, 128), c("sc", 0, 64), 1.0, None, mul)
@@ -344,10 +357,6 @@ def rank_program(g, core, T, topo):
     def setup_s():
         for k in range(16):
             act(k_("bkb", k), c("gmb"), AF.Copy, 0.0, c("R", k, k + 1))
-        for b in (0, 1):
-            w, r = c("pmx", 256 * b, 256 * b + 256), c("bs8", 256 * b, 256 * b + 256)
-            act(r, c("bsel", 256 * b, 256 * b + 256), AF.Copy, 0.0, -8192.0)
-            run("G", lambda w=w, r=r: g.affine_select(ap(w), ap(r), [[-1, 16], [0, 2], [-16, 8]], eq, 0.0, 0, 1), [r], [w], cost=600.0)
         act(THR, TH, AF.Identity, -2048.5, -1.0)
         act(c("gth", 0, 8), c("gc", 0, 8), AF.Copy, 0.0, TH)
         act(c("of32"), c("cI"), AF.Identity, 0.0625, 0.0)
@@ -358,7 +367,8 @@ def rank_program(g, core, T, topo):
         mm(c("pq", 24, 32), c("wn", 128, 256), c("wi", 0, 8), True, True)
         act(c("thc"), c("pq", 0, 16), AF.Identity, 0.75 - (7 - rank) / 16.0)
         act(c("wsc"), c("pq", 16, 32), AF.Identity, -1.21875)
-        act(c("cht"), c("ch"), AF.Identity, 38.185 * LN3, L3)
+        act(c("cht"), c("ch"), AF.Identity, L3)
+        act(c("cno"), c("ch"), AF.Identity, 256.0 - 43.23 - 63 * math.log(2.0), -1.0)
         act(c("ivb"), c("cI"), AF.Copy)
         act(c("cneg"), c("cI"), AF.Identity, -10240.0, 0.0)
         act(c("c16"), c("ck"), AF.Identity, 32768.0, -4096.0)
@@ -384,7 +394,8 @@ def rank_program(g, core, T, topo):
 
     def setup_d():
         ts(c("stmp"), c("tri"), 2.0, None, mul)
-        tt(c("trf"), c("stmp"), c("ih"), sub)
+        tt(c("stmp"), c("stmp"), c("ih"), sub)
+        ts(c("trf"), c("stmp"), 4096.0, None, mul)
 
     def setup_f():
         ts(c("csl", 0, 128), c("cI"), 16.0, -2048.0, mul, add)
@@ -421,24 +432,24 @@ def rank_program(g, core, T, topo):
         for j in range(16):
             mm(c(HB[h], j, 128, 16), c("zf", 2048 * h + j, 2048 * h + 2048, 16), c("ngc", 0, 8), False, j == 15)
 
-    def slots_turn(h, fin, between=None):
+    def slots_turn(h, between=None):
         q = c("qt", 128 * h, 128 * h + 128)
         cp(q, c(HB[h], 0, 128))
-        if fin:
-            mm(c(HB[h], 128, 256), c("ih"), c("k2"), True, False)
-        mm(c(HB[h], 128, 256), q, c("ih"), not fin, True)
+        mm(c(HB[h], 128, 256), q, c("ih"), True, True)
         e = c("em", 128 * h, 128 * h + 128)
-        ts(e, c(HB[h], 128, 256), 2048.0 if fin else 0.0, None, eq)
+        ts(e, c(HB[h], 128, 256), 0.0, None, eq)
         if between:
             between()
         mm(c(HB[h], 256, 384), c("trf"), e, True, True)
 
     def slots_put(h, fin):
         a, b = 128 * h, 128 * h + 128
-        ts(c("fe", a, b), c(HB[h], 256, 384), 0.0, None, lt)
-        tt(c("wmk", a, b), c("fe", a, b), c("npl", a, b), mul)
-        tt(c("yqs" if fin else "qi", a, b), c(HB[h], 128, 256), c("wmk", a, b), add if fin else sub)
-        if not fin:
+        tt(c("fe", a, b), c(HB[h], 256, 384), c("npl", a, b), mx)
+        if fin:
+            tt(c("wmk", a, b), c(HB[h], 128, 256), c("fe", a, b), mi)
+            ts(c("yqs", a, b), c("wmk", a, b), 2048.0, None, add)
+        else:
+            tt(c("qi", a, b), c(HB[h], 128, 256), c("fe", a, b), mi)
             ts(c("ql", a, b), c("qi", a, b), 2048.0, None, add)
 
     def list_queues():
@@ -522,7 +533,7 @@ def rank_program(g, core, T, topo):
         tt(c("cp", 64, 128), c("phi", 0, 64), c("dhi"), add)
         spread("cp", 0, 4)
         if t:
-            slots_turn(0, False, lambda: spread("cp", 4, 8))
+            slots_turn(0, lambda: spread("cp", 4, 8))
         else:
             spread("cp", 4, 8)
         spread("cp", 8, 16)
@@ -534,25 +545,22 @@ def rank_program(g, core, T, topo):
         thermo("S", "dw", 3)
         if t:
             slots_sum(1, False)
+        mm(c("plo", 0, 256), c("on"), c("rho"), True, False)
         for b in (0, 1):
-            mm(c("plo", 0, 256), c("ctb", 128 * b, 128 * b + 128), c("bsel", 256 * b, 256 * b + 256), b == 0, False)
-        mm(c("plo", 0, 256), c("on"), c("rho"), False, False)
+            mm(c("plo", 128 * b, 128 * b + 128), c("ctb", 128 * b, 128 * b + 128), c("on"), False, False)
         for b in (0, 1):
             m = (32, 64)[b]
             z = 2048 * b
             pick("V", "zd", z, z + 16 * m, c("dw"), c("ql", 128 * b, 128 * b + m))
             pick("S", "zd", z + 16 * m, z + 2048, c("dw"), c("ql", 128 * b + m, 128 * b + 128))
             if b == 0 and t:
-                slots_turn(1, False)
+                slots_turn(1)
                 slots_put(1, False)
             for j in range(16):
-                mm(c("plo", 16 * j + 8 * b, 16 * j + 8 * b + 8), c("zd", z + j, z + 2048, 16), c("ngc", 0, 8), False, b == 1 and j == 15)
+                mm(c("plo", 128 * b + j, 128 * b + 128, 16), c("zd", z + j, z + 2048, 16), c("ngc", 0, 8), False, b == 1 and j == 15)
         own = c(land, 16 * rank, 16 * rank + 16)
-        cp(c("tsb", 128, 256), c("plo", 128, 256))
-        tt(c("tm", 0, 128), c("plo", 0, 128), c("tsb", 128, 256), mx)
-        tt(c("tm", 128, 192), c("tm", 0, 64), c("tm", 64, 128), mx)
-        tt(c("tm", 192, 224), c("tm", 128, 160), c("tm", 160, 192), mx)
-        tt(own, c("tm", 192, 208), c("tm", 208, 224), mx)
+        scan(c("tm"), c("rs"), c("plo", 0, 256), mul, mx)
+        cp(own, c("tm", 15, 256, 16))
         src = T[land][:, 16 * rank:16 * rank + 16]
         sem = T.sem["arr%d" % t]
         moves = [RemoteDMATransfer(dst_ids=[did(d) for d in off], dma_engine_mask=sum(1 << e for e in off_e), remote_sem=sem,
@@ -565,7 +573,7 @@ def rank_program(g, core, T, topo):
         arrive = len(off_e) * len(off) + len(near_e) * len(near)
         if t == 0:
             setup_c()
-        cp(c("tsb", 0, 128), c("plo", 0, 128))
+        act(c("tsb"), c("plo", 0, 256), AF.Copy)
         tt(c("x2", 0, 64), c("o", 64, 128), c("o", 0, 64), sub)
         tt(c("x2", 64, 128), c("cp", 64, 128), c("cp", 0, 64), sub)
         ts(c("qa"), c("qi"), 3975, None, OP.bitwise_and)
@@ -578,7 +586,7 @@ def rank_program(g, core, T, topo):
         tt(c("c2", 64, 128), c("cp", 64, 128), c("x2", 192, 256), sub)
         cp(c("ol2"), c("o2"))
         for b in (0, 1):
-            mm(c("phi", 0, 256), c("hfs", 128 * b, 128 * b + 128), c("pmx", 256 * b, 256 * b + 256), b == 0, b == 1)
+            mm(c("phi", 128 * b, 128 * b + 128), c("hfs", 128 * b, 128 * b + 128), c("in8"), True, True)
         mm(c("plo", 0, 128), c("ih"), c("c2"), True, False)
         mm(c("plo", 0, 128), c("ih"), c("emp"), False, False)
         mm(c("plo", 0, 128), c("in8"), c("hm", 128 * t, 128 * t + 128), False, False)
@@ -586,13 +594,12 @@ def rank_program(g, core, T, topo):
         ts(c("p16", 32, 48), own, 1.0, -100.0, lt, mul)
         tt(c("ce", 0, 256), c("phi", 0, 256), c("tsb"), add)
         tt(c("p16", 64, 80), own, c("p16", 32, 48), add)
-        tt(c("ce", 256, 384), c("ce", 0, 128), c("ce", 128, 256), mi)
-        tt(c("ce", 384, 448), c("ce", 256, 320), c("ce", 320, 384), mi)
-        tt(c("ce", 448, 480), c("ce", 384, 416), c("ce", 416, 448), mi)
-        tt(c("p16", 0, 16), c("ce", 448, 464), c("ce", 464, 480), mi)
-        ts(c("p16", 16, 32), c("p16", 0, 16), 1.0, -20000.0, lt, mul)
-        tt(c("p16", 48, 64), c("p16", 0, 16), c("thc"), add)
+        scan(c("ce", 256, 512), c("rb"), c("ce", 0, 256), add, mi)
+        ts(c("p16", 16, 32), c("ce", 271, 512, 16), 1.0, -20000.0, lt, mul)
+        tt(c("p16", 48, 64), c("ce", 271, 512, 16), c("thc"), add)
         tt(c("p16", 80, 96), c("p16", 48, 64), c("p16", 16, 32), add)
+        tt(c("p16", 112, 128), c("p16", 64, 80), c("p16", 80, 96), gt)
+        tt(c("p16", 128, 144), c("p16", 112, 128), c("p16", 64, 80), mul)
         mm(c("phi", 0, 384), c("ih"), c("csl" if last else "cst"), True, False)
         mm(c("r0", 0, 128), c("ih"), c("cneg"), True, False)
         mm(c("r0", 0, 128), c("ih"), c("o2"), False, False)
@@ -607,8 +614,7 @@ def rank_program(g, core, T, topo):
         for b in (0, 1):
             mm(c("pa", 128 * b, 128 * b + 128), c("kb", 128 * b, 128 * b + 128), c("ih"), True, True)
         tt(c("zi"), c("kp"), c("wsc"), add)
-        tt(c("p16", 96, 112), c("kp"), c("p16", 64, 80), eq)
-        tt(c("p16", 112, 128), c("kp"), c("p16", 80, 96), gt)
+        tt(c("p16", 96, 112), c("kp"), c("p16", 128, 144), eq)
         ts(c("ui"), c("zi"), 127, None, OP.bitwise_and)
         ts(c("wm", 0, 256), c("pa", 0, 256), BC, 0.0, add, mx)
         for i in (0, 1):
@@ -616,11 +622,9 @@ def rank_program(g, core, T, topo):
             pick("S", "ze", 1024 * i + 512, 1024 * i + 1024, c("wm"), c("ol2", 64 * i + 32, 64 * i + 64))
             for k in range(16):
                 mm(c("plo", 64 * i, 64 * i + 64), k_("lkb", k), c("ze", 1024 * i + k, 1024 * i + 1024, 16), False, i == 1 and k == 15)
-        tt(c("p16", 128, 144), c("p16", 96, 112), c("p16", 112, 128), mul)
-        ts(c("p16", 128, 144), c("p16", 128, 144), -200.0, 200.0, mul, add)
-        tt(c("p16", 144, 160), c("ui"), c("p16", 128, 144), add)
+        cp(c("p16", 144, 160), c("ui"))
         for i in range(16):
-            ts(k_("oh", i), c("ivb"), c("p16", 144 + i, 145 + i), None, eq)
+            ts(k_("oh", i), c("ivb"), c("p16", 144 + i, 145 + i), c("p16", 96 + i, 97 + i), eq, mul)
         ts(c("st"), c("plo", 0, 128), THR, None, ge)
         mm(c("r0", 0, 128), c("trie"), c("st"), False, True)
         mm(c("phi", 0, 128), c("tri" if last else "trit"), c("st"), False, False)
@@ -648,21 +652,20 @@ def rank_program(g, core, T, topo):
             mm(c("plo", r, 128, 16), k_("fr", r), c("gc", 0, 8), False, r == 15)
         if not last:
             follow()
-        ts(c("lna", 32, 64), c("lna", 0, 32), -35.0, 1000.0, lt, mul)
-        tt(c("lna", 64, 96), c("cht"), c("lna", 0, 32), sub)
+        ts(c("lna", 32, 64), c("pq", 0, 32), 1e-14, None, lt)
+        tt(c("lna", 64, 96), c("lna", 32, 64), c("cno"), mul)
         ts(c("corr"), c("phi", 256, 384), 256.0, None, mi)
-        tt(c("lna", 96, 128), c("lna", 64, 96), c("lna", 32, 64), add)
+        tt(c("lna", 32, 64), c("lna", 64, 96), c("cht"), add)
+        tt(c("lna", 96, 128), c("lna", 32, 64), c("lna", 0, 32), sub)
         ts(c("iseq"), c("phi", 256, 384), 256.0, None, eq)
-        tt(c("lna", 128, 144), c("lna", 96, 128, 2), c("lna", 97, 128, 2), mi)
+        scan(c("lna", 128, 160), c("rb4"), c("lna", 96, 128), add, mi)
         if last:
             tt(c("l16"), c("phi", 128, 256), c("lv"), lt)
         else:
-            act(c("qlw"), c("phi", 128, 256), AF.Relu, 0.0, -1.0)
-        tt(c("lna", 144, 152), c("lna", 128, 144, 2), c("lna", 129, 144, 2), mi)
+            act(c("qlw"), c("phi", 128, 256), AF.Copy)
         if last:
             tt(c("qlw"), c("phi", 128, 256), c("l16"), mul)
-        ts(c("lna", 152, 160), c("lna", 144, 152), 1.0 / LN3, 256.0, mul, mi)
-        ts(c("apf"), c("lna", 152, 160), 12582912.0, 12583168.0, add, sub)
+        ts(c("apf"), c("lna", 131, 160, 4), 12582912.0, 12583168.0, add, sub)
         tt(c("appl"), ind(c("apf"), c("clist", 0, 8)), c("iseq"), mul)
         tt(c("corr"), c("corr"), c("appl"), add)
         act(c("apb"), ind(c("apf"), c("clist", 0, 8)), AF.Copy)
@@ -689,7 +692,7 @@ def rank_program(g, core, T, topo):
                 slots_gather("S", 2 * h + 1)
                 slots_sum(h, True)
             for h in (0, 1):
-                slots_turn(h, True)
+                slots_turn(h)
                 slots_put(h, True)
             run("Y", lambda: g.sync.dma_start(T.yq[:, :], T.yqs[:, :]), [c("yqs")], [], sem="d_yq", inc=16)
     if "order" not in PLAN:

import math
from concourse.bass import DstId, RemoteDMATransfer
from concourse.mybir import AluOpType as OP, ActivationFunctionType as AF

F32, BF, H, I32, U16 = "float32", "bfloat16", "float16", "int32", "uint16"


def _sb(dtype, **names):
    return {n: ("sbuf", [128, w], dtype) for n, w in names.items()}


SCRATCH = {}
SCRATCH.update(_sb(BF, xs=8192, wn=272, gmb=128, lkb=2048, apb=128, bkb=2048, tri=128, i8=128, in8=128, qlm=128, lenm=128,
                   trit=128, cneg=128, c16=128, k2=128, c77=256, trf=128, ihb=128, sm=64, ctb=256, on=128, rho=256,
                   dm=256, ivb=128, hm=384, wg=2048, mn=4096, zd=4096, zf=4096, ze=2048, hfs=256,
                   oh=2048, ub=256))
SCRATCH.update(_sb(I32, oci=128, qsi=256, thi=1, cint=8, qi=256, qa=256, hz=256, hm13=256, zu=32))
SCRATCH.update(_sb(U16, ol=128, ql=256, hu=256, ol2=128, clist=16, ul=16))
SCRATCH.update(_sb(H, ih=128, sh=128, stmp=128, hcb=256, i37=128, pre=128, emp=128, sc=128, trie=128, cst=384, csl=384,
                   k2l=128, o=128, cp=128, c2=128, o2=128, kb=256, st=128, e16=128, fr=2048, o3t=128, tof=128, em=256,
                   qt=256))
SCRATCH.update(_sb(F32, col=32, cI=128, cg=128, ck=128, c8=128, ipm=256, rs=256, rb=256, rb4=32, ch=32, cht=32, cno=32, R=16, n8=128,
                   sx=320, pc=48, of32=128, y1=128, sd=128, dw=2064, fw=2064, tsb=256, tm=256, land0=128, land1=128,
                   land2=128, x2=256, ce=512, p16=160, kt=128, kp=16, wm=272, lna=160, apf=8, qp=128, corr=128, iseq=128,
                   appl=128, qlw=128, l16=128, lv=128, tt=128, wmk=256, npl=256, fe=256, yo=128, yqs=256))
PSUM = ("r0", "r1", "r2", "r3", "pa", "plo", "phi", "pq")
SCRATCH.update({n: ("psum", [128, 512], F32) for n in PSUM})
SEMAPHORES = ["cV", "cS", "cP", "cG", "d_oc", "d_qs", "d_wn", "d_th", "d_x", "d_yo", "d_yq", "arr0", "arr1", "arr2", "loc"]
PART = {"pint": ("cint", 0, 1), "kint": ("cint", 1, 1), "gint": ("cint", 2, 1), "lint": ("cint", 3, 1), "hint": ("cint", 4, 1),
        "dlo": ("sx", 0, 64), "dd": ("sx", 64, 64), "s": ("sx", 128, 64), "ml": ("sx", 192, 64), "dhi": ("sx", 256, 64),
        "gc": ("sm", 0, 16), "ngc": ("sm", 16, 16), "wi": ("sm", 32, 16), "wts": ("sm", 48, 16), "gth": ("pc", 0, 16),
        "thc": ("pc", 16, 16), "wsc": ("pc", 32, 16), "zi": ("zu", 0, 16), "ui": ("zu", 16, 16)}


CYCLE, WAKE, TRIP, SLACK = 1.0, 120.0, 4700.0, 5.0
PLAN = {}


def plan(ops, trips):
    n = len(ops)
    pred = [dict() for _ in range(n)]
    hist, bank = {}, {}
    for i, op in enumerate(ops):
        e = op[0]
        regs = [(False, rg[0], rg[1], rg[2]) for rg in op[2]] + [(True, rg[0], rg[1], rg[2]) for rg in op[3]]
        for wr, b, lo, hi in regs:
            if b in PSUM:
                for k, v in bank.get(b, {}).items():
                    pred[i][v] = max(pred[i].get(v, 0), int(k != e))
            else:
                for a in hist.get(b, []):
                    if a[1] < hi and lo < a[2] and (wr or a[0]):
                        pred[i][a[3]] = 1
        for wr, b, lo, hi in regs:
            if b in PSUM:
                bank.setdefault(b, {})[e] = i
            else:
                h = hist.setdefault(b, [])
                if wr:
                    h[:] = [a for a in h if not (lo <= a[1] and a[2] <= hi)]
                h.append((wr, lo, hi, i))
    for a, b in trips:
        pred[b][a] = 2
    succ = [[] for _ in range(n)]
    for i in range(n):
        for p, k in pred[i].items():
            succ[p].append((i, k))
    way = [0.0] * n
    for i in range(n - 1, -1, -1):
        way[i] = ops[i][6] + max([way[j] + (0, WAKE, TRIP)[k] for j, k in succ[i]] or [0.0])

    def forward(urgent, back):
        after = succ if not back else [list(p.items()) for p in pred]
        before = [list(p.items()) for p in pred] if not back else succ
        left = [len(p) for p in before]
        ready = {e: [i for i in range(n) if ops[i][0] == e and not left[i]] for e in "VSPGY"}
        free, newest, end, order = dict.fromkeys("VSPGY", 0.0), dict.fromkeys("VSPGY", -1), [0.0] * n, []

        def begin(i):
            e = ops[i][0]
            t = free[e]
            for p, k in before[i]:
                if k == 2:
                    t = max(t, end[p] + TRIP)
                elif k == 1 and (end[p] > free[e] or newest[e] == p):
                    t = max(t, end[p] + WAKE)
            return t

        while len(order) < n:
            best = None
            for e in "VSPGY":
                if ready[e]:
                    st = [(begin(i), i) for i in ready[e]]
                    t0 = min(st)[0]
                    t, i = max(((t, i) for t, i in st if t <= t0 + SLACK), key=lambda q: (urgent[q[1]], q[1] if back else -q[1]))
                    if best is None or t < best[0]:
                        best = (t, i, e)
            t, i, e = best
            ready[e].remove(i)
            end[i] = t + ops[i][6]
            free[e] = t + 70 if e == "Y" and not back else end[i]
            newest[e] = i
            order.append(i)
            for j, k in after[i]:
                left[j] -= 1
                if not left[j]:
                    ready[ops[j][0]].append(j)
        return max(end), order, end

    best, urgent = None, way
    for i in range(4):
        total, order, end = forward(urgent, False)
        if best is None or total < best[0]:
            best = (total, order)
        urgent = forward(end, True)[2]
    return best[1]


def rank_program(g, core, T, topo):
    rank = T.rank_of(core)
    if rank is None:
        return
    eng = {"V": g.vector, "S": g.scalar, "P": g.tensor, "G": g, "Y": g.sync}
    count = {"V": 0, "S": 0, "P": 0, "G": 0}
    known = {e: {} for e in eng}
    snap = {}
    ops = []
    trips = []
    hist = {}
    bank = {}

    def wait(e, ev):
        if known[e].get(ev[0], 0) >= ev[1]:
            return
        eng[e].wait_ge(T.sem[ev[0]], ev[1])
        for k, v in list(snap[ev].items()) + [ev]:
            if known[e].get(k, 0) < v:
                known[e][k] = v

    def run(e, fn, reads, writes, sem=None, inc=1, cost=100.0, pre=None):
        ops.append((e, fn, reads, writes, sem, inc, cost, pre))

    def emit(e, fn, reads, writes, sem, inc, cost, pre):
        evs = []
        for wr, regs in ((False, reads), (True, writes)):
            for rg in regs:
                b, lo, hi = rg[0], rg[1], rg[2]
                if b in PSUM:
                    evs += [v for k, v in bank.get(b, {}).items() if k != e]
                else:
                    evs += [a[3] for a in hist.get(b, []) if a[1] < hi and lo < a[2] and (wr or a[0])]
        need = {}
        for k, v in evs:
            need[k] = max(need.get(k, 0), v)
        for ev in sorted(need.items(), key=lambda q: -q[1]):
            wait(e, ev)
        if pre:
            pre()
        if not inc:
            fn()
            return
        if sem is None:
            sem = "c" + e
            count[e] += 1
            ev = (sem, count[e])
        else:
            ev = (sem, inc)
        fn().then_inc(T.sem[sem], inc)
        snap[ev] = dict(known[e])
        for wr, regs in ((False, reads), (True, writes)):
            for rg in regs:
                b, lo, hi = rg[0], rg[1], rg[2]
                if b in PSUM:
                    bank.setdefault(b, {})[e] = ev
                else:
                    h = hist.setdefault(b, [])
                    if wr:
                        h[:] = [a for a in h if not (lo <= a[1] and a[2] <= hi)]
                    else:
                        h[:] = [a for a in h if not (not a[0] and a[3][0] == ev[0] and a[1] == lo and a[2] == hi)]
                    h.append((wr, lo, hi, ev))

    def c(b, lo=None, hi=None, step=1):
        n, at, w = PART.get(b) or (b, 0, SCRATCH[b][1][1])
        if lo is None:
            lo, hi = 0, w
        return (n, at + lo, at + hi, step)

    def ap(x):
        if x[0] == "ind":
            return ap(x[1]).indirect(ap(x[2]))
        return T[x[0]][:, x[1]:x[2]:x[3]] if x[3] != 1 else T[x[0]][:, x[1]:x[2]]

    def ind(w, o):
        return ("ind", w, o)

    def rd(*xs):
        out = []
        for x in xs:
            if isinstance(x, tuple):
                out += [x[1], x[2]] if x[0] == "ind" else [x]
        return out

    def val(x):
        return ap(x) if isinstance(x, tuple) else x

    def wide(x):
        return 16 * (x[2][2] - x[2][1]) if x[0] == "ind" else -(-(x[2] - x[1]) // x[3])

    def took(out, *ins):
        if any(x[0] == "ind" for x in ins):
            return 50 + 1.56 * CYCLE * wide(out)
        small = all(SCRATCH[x[0]][2] in (BF, H, U16) for x in (out,) + ins)
        both = len(ins) == 2 and not any(x[0] in PSUM for x in ins)
        return CYCLE * max(64, wide(out) * (2 if both else 0.5 if small and len(ins) == 1 else 1))

    def ts(out, a, s1, s2, o0, o1=None):
        if o1 is None:
            run("V", lambda: g.vector.tensor_scalar(ap(out), ap(a), val(s1), None, o0), rd(a, s1), [out], cost=took(out, a))
        else:
            run("V", lambda: g.vector.tensor_scalar(ap(out), ap(a), val(s1), val(s2), o0, o1), rd(a, s1, s2), [out], cost=took(out, a))

    def tt(out, a, b, op):
        run("V", lambda: g.vector.tensor_tensor(ap(out), ap(a), ap(b), op), rd(a, b), [out], cost=took(out, a, b))

    def cp(out, a):
        run("V", lambda: g.vector.tensor_copy(ap(out), ap(a)), rd(a), [out], cost=took(out, a))

    def scan(out, d0, d1, o0, o1):
        run("V", lambda: g.vector.tensor_tensor_scan(ap(out), ap(d0), ap(d1), 0.0, o0, o1), rd(d0, d1), [out], cost=CYCLE * max(64, wide(out)))

    def fill(out, v):
        run("V", lambda: g.vector.memset(ap(out), v), [], [out], cost=took(out))

    def act(out, a, func, bias=0.0, scale=1.0):
        cost = 65 + 1.56 * CYCLE * wide(out) if a[0] == "ind" else CYCLE * max(64, wide(out))
        run("S", lambda: g.scalar.activation(ap(out), ap(a), func, bias=val(bias), scale=val(scale)), rd(a, bias, scale), [out],
            cost=cost + (1300 if func == AF.Exp else 0))

    def mm(out, l, r, start, stop):
        run("P", lambda: g.tensor.matmul(ap(out), ap(l), ap(r), start, stop), rd(l, r), [out],
            cost=CYCLE * max(min(64, wide(l)), wide(r)) * (4 if SCRATCH[l[0]][2] == F32 else 1))

    def iota(out, pattern, base, cm):
        cost = 130 + 2 * CYCLE * wide(out)
        if SCRATCH[out[0]][2] != I32:
            run("G", lambda: g.iota(ap(out), pattern, base, cm, allow_small_or_imprecise_dtypes=True), [], [out], cost=cost)
        else:
            run("G", lambda: g.iota(ap(out), pattern, base, cm), [], [out], cost=cost)

    def load(e, sem, b, hi, src):
        run(e, lambda: eng[e].dma_start(T[b][:, 0:hi], src), [], [c(b, 0, hi)], sem=sem, inc=16, cost=9000.0 if b == "xs" else 2000.0)

    def k_(b, k):
        return c(b, 128 * k, 128 * k + 128)

    PC, KC, GC, K8, BC, TH, THR, P64, W64, WX, PP, L3, LN, KX = [c("col", i, i + 1) for i in range(14)]
    add, sub, mul, mx, mi, eq, ge, gt, lt = (OP.add, OP.subtract, OP.mult, OP.max, OP.min, OP.is_equal, OP.is_ge, OP.is_gt, OP.is_lt)

    load("Y", "d_oc", "oci", 128, T.oc[:, :])
    load("Y", "d_wn", "wn", 256, T.want[:, :])
    load("Y", "d_x", "xs", 8192, T.x[:, :])
    load("Y", "d_qs", "qsi", 256, T.qs[:, :])
    load("Y", "d_th", "thi", 1, T.th[:, :])

    iota(c("pint"), [[0, 1]], 0, 1)
    iota(c("cI"), [[1, 128]], 0, 0)
    iota(PC, [[0, 1]], 0, 1)
    iota(c("cg"), [[1, 8], [0, 16]], 0, 0)
    iota(c("ck"), [[0, 8], [1, 16]], 0, 0)
    iota(c("c8"), [[0, 16], [1, 8]], 0, 0)
    iota(c("ch"), [[0, 8], [64, 4]], 0, 0)
    iota(c("ipm"), [[1, 256]], -256, 0)

    fill(c("wn", 256, 272), 0.0)
    fill(c("lkb"), 0.0)
    fill(LN, math.exp(43.23))
    fill(c("dw", 2048, 2064), 0.0)
    fill(c("wm", 256, 272), 0.0)
    ts(c("kint"), c("pint"), 15, None, OP.bitwise_and)
    ts(c("gint"), c("pint"), 4, None, OP.arith_shift_right)
    ts(c("lint"), c("pint"), 63, None, OP.bitwise_and)
    ts(c("hint"), c("pint"), 6, None, OP.arith_shift_right)
    cp(KC, c("kint"))
    cp(GC, c("gint"))
    cp(P64, c("lint"))
    cp(W64, c("hint"))
    ts(c("gmb"), c("cg"), GC, None, eq)
    ts(c("ih"), c("cI"), PC, None, eq)
    ts(c("R"), c("cI", 0, 16), KC, None, eq)
    ts(K8, KC, 0.125, None, mul)
    ts(c("stmp"), c("cI"), 1.0, PC, sub, eq)
    ts(c("hcb", 0, 128), c("cI"), c("R", 0, 1), 8.5, mul, add)
    ts(c("hcb", 128, 256), c("cI"), 0.0, -0.46875, mul, add)
    tt(c("sh"), c("stmp"), c("gmb"), mul)
    ts(c("i37"), c("ih"), 37.0, None, mul)
    ts(c("n8"), c("cI"), 2.0, K8, mul, add)
    cp(c("o"), c("oci"))
    cp(c("ol"), c("oci"))
    act(WX, P64, AF.Exp, 43.0, -1.0)
    act(L3, LN, AF.Ln)
    for k in range(16):
        act(c("lkb", 128 * k + k, 128 * k + 128, 16), c("gmb", k, 128, 16), AF.Copy)
    ts(c("pre"), c("cI"), 0.0, -2047.0, mul, add)

    def h_consts(t):
        mm(c("pa", 0, 256), c("ih"), c("hcb"), True, False)
        if t:
            mm(c("pa", 128, 256), c("ih"), c("c77", 128 * (t - 1), 128 * t), False, False)

    def h_data():
        mm(c("pa", 0, 128), c("sh"), c("o"), False, False)
        mm(c("pa", 128, 256), c("i37"), c("o"), False, True)

    def empties():
        ts(c("emp"), c("o"), 256.0, -8192.0, ge, mul)

    h_consts(0)
    h_data()

    def offsets():
        tt(c("y1"), c("pa", 0, 128), c("n8"), mul)
        for i in (0, 1):
            q, a = 64 * i, 128 * i
            tt(c("hz", a, a + 64), c("y1", q, q + 64), c("pa", 128 + q, 192 + q), add)
            tt(c("hz", a + 64, a + 128), c("y1", 64 - q, 128 - q), c("pa", 128 + q, 192 + q), add)
            ts(c("hm13", a, a + 128), c("hz", a, a + 128), 8191, None, OP.bitwise_and)
            cp(c("hu", a, a + 128), c("hm13", a, a + 128))

    def setup_b():
        ts(c("qa"), c("qsi"), 15, None, OP.bitwise_and)
        ts(c("hm13"), c("qsi"), 4, None, OP.arith_shift_right)
        ts(c("qi"), c("qsi"), 2048.0, 1920.0, ge, mul)
        ts(c("qa"), c("qa"), 128.0, None, mul)
        tt(c("hm13"), c("hm13"), c("qi"), add)
        tt(c("qi"), c("qa"), c("hm13"), add)
        cp(c("ql"), c("qi"))
        ts(BC, KC, -256.0, 2048.0, mul, add)
        ts(KX, KC, 16.0, None, mul)
        cp(TH, c("thi"))
        cp(c("gc", 0, 8), c("gmb", 0, 128, 16))
        ts(c("ngc", 0, 8), c("gc", 0, 8), -1.0, None, mul)
        ts(c("ctb", 0, 128), c("cI"), 32.0, 32.0, ge, mul)
        ts(c("ctb", 128, 256), c("cI"), 64.0, 32.0, ge, mul)
        fill(c("on"), 1.0)
        fill(c("rho"), (7 - rank) / 2048.0)
        for b in (0, 1):
            ts(c("rs", 128 * b, 128 * b + 128), c("ck"), 0.0, None, gt)
            ts(c("rb", 128 * b, 128 * b + 128), c("ck"), 0.0, 1e5, eq, mul)
        ts(c("rb4"), c("ch"), 0.0, 1e5, eq, mul)
        ts(c("clist"), c("cI", 0, 16), 0.0, None, add)
        ts(c("sc"), c("cI"), 32.0, -4096.0, ge, mul)
        ts(c("sc", 64, 128), c("sc", 0, 64), 1.0, None, mul)
        for t in range(3):
            ts(c("hm", 128 * t, 128 * t + 128), c("c8"), float(t), c("R", 0, 1), eq, mul)

    def setup_s():
        for k in range(16):
            act(k_("bkb", k), c("gmb"), AF.Copy, 0.0, c("R", k, k + 1))
        act(THR, TH, AF.Identity, -2048.5, -1.0)
        act(c("gth", 0, 8), c("gc", 0, 8), AF.Copy, 0.0, TH)
        act(c("of32"), c("cI"), AF.Identity, 0.0625, 0.0)
        act(c("wi", 0, 8), c("gc", 0, 8), AF.Copy, 0.0, KX)
        mm(c("pq", 0, 8), c("of32"), c("gth", 0, 8), True, True)
        mm(c("pq", 8, 16), c("of32"), c("gth", 0, 8), True, True)
        mm(c("pq", 16, 24), c("wn", 0, 128), c("wi", 0, 8), True, True)
        mm(c("pq", 24, 32), c("wn", 128, 256), c("wi", 0, 8), True, True)
        act(c("thc"), c("pq", 0, 16), AF.Identity, 0.75 - (7 - rank) / 16.0)
        act(c("wsc"), c("pq", 16, 32), AF.Identity, -1.21875)
        act(c("cht"), c("ch"), AF.Identity, L3)
        act(c("cno"), c("ch"), AF.Identity, 256.0 - 43.23 - 63 * math.log(2.0), -1.0)
        act(c("ivb"), c("cI"), AF.Copy)
        act(c("cneg"), c("cI"), AF.Identity, -10240.0, 0.0)
        act(c("c16"), c("ck"), AF.Identity, 32768.0, -4096.0)
        act(c("k2"), c("cI"), AF.Identity, 2048.0, 0.0)
        act(c("c77", 0, 128), c("cI"), AF.Identity, 77.0, 0.0)
        act(c("c77", 128, 256), c("cI"), AF.Identity, 154.0, 0.0)
        act(c("fw", 2048, 2064), c("dw", 2048, 2064), AF.Relu, BC)
        act(c("qlm"), c("gmb"), AF.Copy, 0.0, 128.0)
        act(c("lenm"), c("gmb"), AF.Copy, 0.0, -256.0)
        act(c("in8"), c("ihb"), AF.Copy, 0.0, -8192.0)
        act(c("i8"), c("ihb"), AF.Copy, 0.0, 8192.0)
        act(c("trit"), c("tri"), AF.Copy, 0.0, 128.0)

    def setup_c():
        ts(c("stmp"), c("tri"), 256.0, None, mul)
        tt(c("trie"), c("stmp"), c("i8"), add)
        ts(c("cst", 0, 128), c("cI"), 2048.0, None, sub)
        ts(c("cst", 128, 256), c("cI"), 2048.0, None, sub)
        ts(c("cst", 256, 384), c("ck"), 256.0, 256.0, mul, add)
        ts(c("dm", 0, 128), c("ck"), KC, None, eq)
        ts(c("dm", 128, 256), c("ck"), KC, None, eq)
        ts(c("wts", 0, 2), c("cI", 0, 2), W64, WX, eq, mul)

    def setup_d():
        ts(c("stmp"), c("tri"), 2.0, None, mul)
        tt(c("stmp"), c("stmp"), c("ih"), sub)
        ts(c("trf"), c("stmp"), 4096.0, None, mul)

    def setup_f():
        ts(c("csl", 0, 128), c("cI"), 16.0, -2048.0, mul, add)
        ts(c("csl", 128, 256), c("cI"), 16.0, -2048.0, mul, add)
        ts(c("csl", 256, 384), c("ck"), 256.0, 256.0, mul, add)
        ts(c("lv"), c("cI"), 16.0, -2032.0, mul, add)
        ts(PP, PC, 64.0, 4096.0, ge, mul)
        ts(c("k2l"), c("cI"), 0.0, PP, mul, add)
        ts(c("k2l"), c("k2l"), 2048.0, None, sub)

    def spread(src, k0, k1):
        for k in range(k0, k1):
            mm(c("r%d" % (k // 4), 128 * (k % 4), 128 * (k % 4) + 128), k_("bkb", k), c(src), True, True)

    def thermo(e, dst, i):
        if e == "V":
            ts(c(dst, 512 * i, 512 * i + 512), c("r%d" % i), BC, 0.0, add, mx)
        else:
            act(c(dst, 512 * i, 512 * i + 512), c("r%d" % i), AF.Relu, BC)

    def pick(e, z, a, b, win, off):
        if e == "V":
            ts(c(z, a, b), ind(win, off), -1.0, -256.0, mul, mx)
        else:
            act(c(z, a, b), ind(win, off), AF.Relu, 256.0, -1.0)

    def slots_gather(e, i):
        pick(e, "zf", 1024 * i, 1024 * i + 1024, c("fw"), c("ql", 64 * i, 64 * i + 64))

    HB = ("pa", "pq")

    def slots_sum(h, fin):
        mm(c(HB[h], 0, 128), c("ih"), c("k2l" if fin else "k2"), True, False)
        for j in range(16):
            mm(c(HB[h], j, 128, 16), c("zf", 2048 * h + j, 2048 * h + 2048, 16), c("ngc", 0, 8), False, j == 15)

    def slots_turn(h, between=None):
        q = c("qt", 128 * h, 128 * h + 128)
        cp(q, c(HB[h], 0, 128))
        mm(c(HB[h], 128, 256), q, c("ih"), True, True)
        e = c("em", 128 * h, 128 * h + 128)
        ts(e, c(HB[h], 128, 256), 0.0, None, eq)
        if between:
            between()
        mm(c(HB[h], 256, 384), c("trf"), e, True, True)

    def slots_put(h, fin):
        a, b = 128 * h, 128 * h + 128
        tt(c("fe", a, b), c(HB[h], 256, 384), c("npl", a, b), mx)
        if fin:
            tt(c("wmk", a, b), c(HB[h], 128, 256), c("fe", a, b), mi)
            ts(c("yqs", a, b), c("wmk", a, b), 2048.0, None, add)
        else:
            tt(c("qi", a, b), c(HB[h], 128, 256), c("fe", a, b), mi)
            ts(c("ql", a, b), c("qi", a, b), 2048.0, None, add)

    def list_queues():
        mm(c("pq", 128, 256), c("apb"), c("ih"), True, True)
        tt(c("ub"), ind(c("ui"), c("clist")), c("dm"), mul)
        for b in (0, 1):
            mm(c("pq", 64 + 8 * b, 72 + 8 * b), c("ub", 128 * b, 128 * b + 128), c("gc", 0, 8), True, True)

    def applied():
        cp(c("qp"), c("pq", 128, 256))
        cp(c("ul"), c("pq", 64, 80))

    def appended():
        tt(c("wmk"), ind(c("qp"), c("ul")), c("ipm"), eq)
        tt(c("npl"), ind(c("qlw"), c("ul")), c("wmk"), mul)

    off = [d for d in T.cores if d != core and topo.chip(d) != topo.chip(core)]
    near = [d for d in T.cores if d != core and topo.chip(d) == topo.chip(core)]
    off_e = sorted(set(e for d in off for e in topo.engines(core, d)))
    near_e = [e for d in near for e in topo.engines(core, d) if e not in off_e]

    def did(d):
        a = topo.addr(d)
        return DstId(rid=a[0], pnc=a[1])

    def sums(b, a, z0, stop=True):
        for k in range(16):
            mm(c(b, a, a + 64), k_("lkb", k), c("mn", z0 + k, z0 + 1024, 16), False, stop and k == 15)

    for t in range(3):
        last = t == 2
        land = "land%d" % t
        for i in (0, 1):
            act(c("wg", 1024 * i, 1024 * i + 1024), ind(c("wn"), c("ol", 64 * i, 64 * i + 64)), AF.Copy)
        if t == 0:
            offsets()
            empties()
            cp(c("ihb"), c("ih"))
            ts(c("stmp"), c("cI"), PC, None, gt)
            tt(c("tri"), c("stmp"), c("gmb"), mul)
            setup_b()
            setup_s()
        else:
            for i in range(4):
                thermo("S", "fw", i)
            for i in range(4):
                slots_gather("S", i)
        mm(c("plo", 0, 128), c("ih"), c("pre"), True, False)
        mm(c("plo", 64, 128), c("ih"), c("emp", 0, 64), False, False)
        mm(c("phi", 0, 64), c("ih"), c("pre", 0, 64), True, False)

        def records(i, other):
            a = 2048 * i + 1024 * other
            tt(c("mn", a, a + 1024), ind(c("xs"), c("hu", 128 * i + 64 * other, 128 * i + 64 * other + 64)),
               c("wg", 1024 * i, 1024 * i + 1024), mi)
            return a

        sums("plo", 0, records(0, 0), False)
        if t:
            list_queues()
        sums("plo", 64, records(0, 1))
        mm(c("r3", 0, 64), c("ih"), c("emp", 64, 128), True, False)
        mm(c("r3", 0, 64), c("ih"), c("pre", 0, 64), False, False)
        sums("phi", 0, records(1, 0))
        if t == 1:
            setup_f()
        cp(c("ml"), c("plo", 0, 64))
        tt(c("dlo"), c("plo", 64, 128), c("ml"), sub)
        sums("r3", 0, records(1, 1))
        if t:
            applied()
            appended()
            slots_sum(0, False)
        cp(c("sd", 64, 128), c("phi", 0, 64))
        tt(c("dhi"), c("r3", 0, 64), c("sd", 64, 128), sub)
        tt(c("dd"), c("dhi"), c("dlo"), add)
        ts(c("s"), c("dd"), 0.0, None, gt)
        tt(c("dlo"), c("s"), c("dlo"), mul)
        tt(c("dhi"), c("s"), c("dhi"), mul)
        tt(c("cp", 0, 64), c("ml"), c("dlo"), add)
        tt(c("cp", 64, 128), c("phi", 0, 64), c("dhi"), add)
        spread("cp", 0, 4)
        if t:
            slots_turn(0, lambda: spread("cp", 4, 8))
        else:
            spread("cp", 4, 8)
        spread("cp", 8, 16)
        thermo("V", "dw", 0)
        if t:
            slots_put(0, False)
        thermo("V", "dw", 2)
        thermo("S", "dw", 1)
        thermo("S", "dw", 3)
        if t:
            slots_sum(1, False)
        mm(c("plo", 0, 256), c("on"), c("rho"), True, False)
        for b in (0, 1):
            mm(c("plo", 128 * b, 128 * b + 128), c("ctb", 128 * b, 128 * b + 128), c("on"), False, False)
        for b in (0, 1):
            m = (32, 64)[b]
            z = 2048 * b
            pick("V", "zd", z, z + 16 * m, c("dw"), c("ql", 128 * b, 128 * b + m))
            pick("S", "zd", z + 16 * m, z + 2048, c("dw"), c("ql", 128 * b + m, 128 * b + 128))
            if b == 0 and t:
                slots_turn(1)
                slots_put(1, False)
            for j in range(16):
                mm(c("plo", 128 * b + j, 128 * b + 128, 16), c("zd", z + j, z + 2048, 16), c("ngc", 0, 8), False, b == 1 and j == 15)
        own = c(land, 16 * rank, 16 * rank + 16)
        scan(c("tm"), c("rs"), c("plo", 0, 256), mul, mx)
        cp(own, c("tm", 15, 256, 16))
        src = T[land][:, 16 * rank:16 * rank + 16]
        sem = T.sem["arr%d" % t]
        moves = [RemoteDMATransfer(dst_ids=[did(d) for d in off], dma_engine_mask=sum(1 << e for e in off_e), remote_sem=sem,
                                   srcs=[src], dsts=[src for d in off])]
        if near:
            moves.append(RemoteDMATransfer(dst_ids=[did(d) for d in near], dma_engine_mask=sum(1 << e for e in near_e),
                                           remote_sem=sem, srcs=[src], dsts=[src for d in near]))
        run("G", lambda moves=moves: g.remote_dma_fused(moves, local_sem=T.sem.loc), [own], [], inc=0, cost=300.0)
        sent = len(ops) - 1
        arrive = len(off_e) * len(off) + len(near_e) * len(near)
        if t == 0:
            setup_c()
        act(c("tsb"), c("plo", 0, 256), AF.Copy)
        tt(c("x2", 0, 64), c("o", 64, 128), c("o", 0, 64), sub)
        tt(c("x2", 64, 128), c("cp", 64, 128), c("cp", 0, 64), sub)
        ts(c("qa"), c("qi"), 3975, None, OP.bitwise_and)
        tt(c("x2", 128, 192), c("x2", 0, 64), c("s"), mul)
        tt(c("x2", 192, 256), c("x2", 64, 128), c("s"), mul)
        ts(c("hfs"), c("qa"), float(t + (2048 if t else 0)), None, eq)
        tt(c("o2", 0, 64), c("o", 0, 64), c("x2", 128, 192), add)
        tt(c("o2", 64, 128), c("o", 64, 128), c("x2", 128, 192), sub)
        tt(c("c2", 0, 64), c("cp", 0, 64), c("x2", 192, 256), add)
        tt(c("c2", 64, 128), c("cp", 64, 128), c("x2", 192, 256), sub)
        cp(c("ol2"), c("o2"))
        for b in (0, 1):
            mm(c("phi", 128 * b, 128 * b + 128), c("hfs", 128 * b, 128 * b + 128), c("in8"), True, True)
        mm(c("plo", 0, 128), c("ih"), c("c2"), True, False)
        mm(c("plo", 0, 128), c("ih"), c("emp"), False, False)
        mm(c("plo", 0, 128), c("in8"), c("hm", 128 * t, 128 * t + 128), False, False)
        mm(c("plo", 0, 128), c("ih"), c("sc"), False, False)
        ts(c("p16", 32, 48), own, 1.0, -100.0, lt, mul)
        tt(c("ce", 0, 256), c("phi", 0, 256), c("tsb"), add)
        tt(c("p16", 64, 80), own, c("p16", 32, 48), add)
        scan(c("ce", 256, 512), c("rb"), c("ce", 0, 256), add, mi)
        ts(c("p16", 16, 32), c("ce", 271, 512, 16), 1.0, -20000.0, lt, mul)
        tt(c("p16", 48, 64), c("ce", 271, 512, 16), c("thc"), add)
        tt(c("p16", 80, 96), c("p16", 48, 64), c("p16", 16, 32), add)
        tt(c("p16", 112, 128), c("p16", 64, 80), c("p16", 80, 96), gt)
        tt(c("p16", 128, 144), c("p16", 112, 128), c("p16", 64, 80), mul)
        mm(c("phi", 0, 384), c("ih"), c("csl" if last else "cst"), True, False)
        mm(c("r0", 0, 128), c("ih"), c("cneg"), True, False)
        mm(c("r0", 0, 128), c("ih"), c("o2"), False, False)
        if t == 0:
            setup_d()
        tt(c("kt", 0, 64), c(land, 0, 64), c(land, 64, 128), mx)
        ops[-1] = ops[-1][:7] + (lambda sem=sem, n=arrive: g.vector.wait_ge(sem, n),)
        trips.append((sent, len(ops) - 1))
        tt(c("kt", 64, 96), c("kt", 0, 32), c("kt", 32, 64), mx)
        tt(c("kp"), c("kt", 64, 80), c("kt", 80, 96), mx)
        ts(c("kb"), ind(c("kp"), c("clist")), -2048.21875, None, add)
        for b in (0, 1):
            mm(c("pa", 128 * b, 128 * b + 128), c("kb", 128 * b, 128 * b + 128), c("ih"), True, True)
        tt(c("zi"), c("kp"), c("wsc"), add)
        tt(c("p16", 96, 112), c("kp"), c("p16", 128, 144), eq)
        ts(c("ui"), c("zi"), 127, None, OP.bitwise_and)
        ts(c("wm", 0, 256), c("pa", 0, 256), BC, 0.0, add, mx)
        for i in (0, 1):
            pick("V", "ze", 1024 * i, 1024 * i + 512, c("wm"), c("ol2", 64 * i, 64 * i + 32))
            pick("S", "ze", 1024 * i + 512, 1024 * i + 1024, c("wm"), c("ol2", 64 * i + 32, 64 * i + 64))
            for k in range(16):
                mm(c("plo", 64 * i, 64 * i + 64), k_("lkb", k), c("ze", 1024 * i + k, 1024 * i + 1024, 16), False, i == 1 and k == 15)
        cp(c("p16", 144, 160), c("ui"))
        for i in range(16):
            ts(k_("oh", i), c("ivb"), c("p16", 144 + i, 145 + i), c("p16", 96 + i, 97 + i), eq, mul)
        ts(c("st"), c("plo", 0, 128), THR, None, ge)
        mm(c("r0", 0, 128), c("trie"), c("st"), False, True)
        mm(c("phi", 0, 128), c("tri" if last else "trit"), c("st"), False, False)
        mm(c("phi", 128, 256), c("gmb" if last else "qlm"), c("st"), False, False)
        mm(c("phi", 256, 384), c("st"), c("lenm"), False, True)
        mm(c("plo", 0, 128), c("ih"), c("c16"), True, False)
        for i in range(16):
            b, h = i // 8, i % 8
            mm(c("pq", 4 * h + 2 * b, 4 * h + 2 * b + 2), k_("oh", i), c("wts", 0, 2), True, True)
        act(c("lna", 0, 32), c("pq", 0, 32), AF.Ln, 2.0 ** -63)
        cp(c("e16"), c("r0", 0, 128))

        def follow():
            tt(c("tt"), c("phi", 0, 128), c("st"), mul)
            tt(c("x2", 0, 64), c("tt", 64, 128), c("tt", 0, 64), sub)
            tt(c("x2", 64, 128), c("x2", 0, 64), c("s"), mul)
            tt(c("tof", 0, 64), c("tt", 0, 64), c("x2", 64, 128), add)
            tt(c("tof", 64, 128), c("tt", 64, 128), c("x2", 64, 128), sub)

        if last:
            follow()
            spread("tof", 0, 16)
        for r in range(16):
            ts(k_("fr", r), c("e16"), 256.0 * r - 2048.0, 256.0 * r - 1792.0, mx, mi)
            mm(c("plo", r, 128, 16), k_("fr", r), c("gc", 0, 8), False, r == 15)
        if not last:
            follow()
        ts(c("lna", 32, 64), c("pq", 0, 32), 1e-14, None, lt)
        tt(c("lna", 64, 96), c("lna", 32, 64), c("cno"), mul)
        ts(c("corr"), c("phi", 256, 384), 256.0, None, mi)
        tt(c("lna", 32, 64), c("lna", 64, 96), c("cht"), add)
        tt(c("lna", 96, 128), c("lna", 32, 64), c("lna", 0, 32), sub)
        ts(c("iseq"), c("phi", 256, 384), 256.0, None, eq)
        scan(c("lna", 128, 160), c("rb4"), c("lna", 96, 128), add, mi)
        if last:
            tt(c("l16"), c("phi", 128, 256), c("lv"), lt)
        else:
            act(c("qlw"), c("phi", 128, 256), AF.Copy)
        if last:
            tt(c("qlw"), c("phi", 128, 256), c("l16"), mul)
        ts(c("apf"), c("lna", 131, 160, 4), 12582912.0, 12583168.0, add, sub)
        tt(c("appl"), ind(c("apf"), c("clist", 0, 8)), c("iseq"), mul)
        tt(c("corr"), c("corr"), c("appl"), add)
        act(c("apb"), ind(c("apf"), c("clist", 0, 8)), AF.Copy)
        tt(c("o3t"), c("plo", 0, 128), c("corr"), add)
        mm(c("plo", 128, 256), c("o3t"), c("ih"), True, True)
        if not last:
            h_consts(t + 1)
            cp(c("o"), c("plo", 128, 256))
            cp(c("ol"), c("plo", 128, 256))
            h_data()
            spread("tof", 0, 16)
            offsets()
            empties()
        else:
            cp(c("yo"), c("plo", 128, 256))
            run("Y", lambda: g.sync.dma_start(T.yoc[:, :], T.yo[:, :]), [c("yo")], [], sem="d_yo", inc=16)
            list_queues()
            for i in range(4):
                thermo("VS"[i & 1], "fw", i)
            applied()
            appended()
            for h in (0, 1):
                slots_gather("V", 2 * h)
                slots_gather("S", 2 * h + 1)
                slots_sum(h, True)
            for h in (0, 1):
                slots_turn(h)
                slots_put(h, True)
            run("Y", lambda: g.sync.dma_start(T.yq[:, :], T.yqs[:, :]), [c("yqs")], [], sem="d_yq", inc=16)
    if "order" not in PLAN:
        PLAN["order"] = plan(ops, trips)
    for i in PLAN["order"]:
        emit(*ops[i])
    g.sync.wait_ge(T.sem.d_yo, 16)
    g.sync.wait_ge(T.sem.d_yq, 16)
    for e in ("V", "S", "P", "G"):
        g.wait_ge(T.sem["c" + e], count[e])
    g.wait_ge(T.sem.loc, 3 * (len(off_e) + (len(near_e) if near else 0)))
